import numpy as np
import ml_dtypes


def mxq(x, axis, fmt="e4m3"):
    dtype, down = {"e4m3": (ml_dtypes.float8_e4m3fn, 7), "e5m2": (ml_dtypes.float8_e5m2, 14)}[fmt]
    v = np.moveaxis(np.asarray(x, np.float32).astype(ml_dtypes.bfloat16).astype(np.float64), axis, -1)
    blocks = v.reshape(v.shape[:-1] + (-1, 32))
    amax = np.abs(blocks).max(-1, keepdims=True)
    byte = np.maximum(np.where(amax > 0, np.frexp(amax)[1] - 1 + 127, 0) - down, 1)
    scale = np.exp2(byte - 127.0)
    codes = (blocks / scale).astype(np.float32).astype(dtype).astype(np.float64)
    return np.moveaxis((codes * scale).reshape(v.shape), -1, axis)


WIDE = False


def mx_kscale(k):
    if not WIDE:
        return np.ones(k)
    levels = np.array([10, -10, 5, -5, 0])
    if k % 512:
        return np.exp2(np.random.permutation(np.resize(levels, k // 32))).repeat(32)
    a = np.empty((k // 512, 16))
    for p in range(k // 512):
        a[p, :8] = np.random.permutation(np.resize(levels, 8))
        for g in range(8):
            far = levels[np.abs(levels - a[p, g]) >= 10]
            a[p, g + 8] = far[np.random.randint(len(far))]
    return np.exp2(a.ravel()).repeat(32)


def f64(x):
    return np.asarray(x).astype(np.float64)


def striped(idx):
    return np.tile(idx.reshape(-1, 16).T, (8, 1)).astype(np.uint16)


def unstriped(offs):
    return offs[:16].T.reshape(-1).astype(np.int64)


E2M1 = np.array([0.0, 0.5, 1.0, 1.5, 2.0, 3.0, 4.0, 6.0, -0.0, -0.5, -1.0, -1.5, -2.0, -3.0, -4.0, -6.0])


def pack_weight(w, fmt):
    k, n = w.shape
    w = f64(np.asarray(w, np.float32).astype(ml_dtypes.bfloat16)).reshape(k // 32, 32, n)
    amax = np.abs(w).max(1)
    if fmt == "e4m3":
        byte = np.frexp(amax)[1] - 1 + 127 - 7
    else:
        mant, ex = np.frexp(amax / 6.0)
        byte = np.where(mant > 0.5, ex, ex - 1) + 127
    byte = np.clip(np.where(amax > 0, byte, 1), 1, 254)
    scaled = (w * np.exp2(127.0 - byte)[:, None, :]).reshape(k, n).astype(np.float32)
    by_word = np.ascontiguousarray(scaled.reshape(k // 512, 128, 4, n).transpose(0, 1, 3, 2))
    if fmt == "e4m3":
        words = by_word.astype(ml_dtypes.float8_e4m3fn).view(np.uint8)
    else:
        c = by_word.astype(ml_dtypes.float4_e2m1fn).view(np.uint8) & 0xF
        words = (c[..., 0::2] | (c[..., 1::2] << 4)).reshape(k // 512, 128, 2 * n)
    return np.ascontiguousarray(words), np.ascontiguousarray(byte.astype(np.uint8).reshape(k // 512, 16, n))


def unpack_weight(words, scales, fmt):
    g, _, n = scales.shape
    words = np.ascontiguousarray(words).reshape(g, 128, n, -1)
    if fmt == "e4m3":
        vals = words.view(ml_dtypes.float8_e4m3fn).astype(np.float64)
    else:
        nib = np.empty((g, 128, n, 4), np.uint8)
        nib[..., 0::2] = words & 0xF
        nib[..., 1::2] = words >> 4
        vals = E2M1[nib]
    vals = vals * np.repeat(np.exp2(scales.astype(np.float64) - 127.0), 8, axis=1)[..., None]
    return vals.transpose(0, 1, 3, 2).reshape(g * 512, n)


def d_relu2(v):
    return 2.0 * np.maximum(v, 0.0)


K, T, E, C, H, N = 512, 512, 8, 128, 512, 1024


def by_expert(wq, xq):
    return np.concatenate([wq[e].T @ xq[:, e * C:(e + 1) * C] for e in range(E)], axis=1)


def setup_inputs():
    n = np.random.standard_normal
    s = mx_kscale(K)
    v = mx_kscale(N)
    u = mx_kscale(H)
    first = np.random.permutation(np.repeat(np.arange(E), T // E))
    second = (first + 1 + np.random.permutation(np.repeat(np.arange(E - 1), -(-T // (E - 1)))[:T])) % E
    while np.bincount(second, minlength=E).max() != T // E:
        load = np.bincount(second, minlength=E); hi, lo = int(load.argmax()), int(load.argmin())
        t = np.flatnonzero((second == hi) & (first != lo))[0]; second[t] = lo
    slot_token = np.empty(E * C, np.int64); pos = np.empty((2, T), np.int64); fill = np.zeros(E, np.int64)
    place = np.stack([np.random.permutation(C) for _ in range(E)])
    for r, deal in enumerate((first, second)):
        for t in np.random.permutation(T):
            e = deal[t]; j = e * C + place[e, fill[e]]; fill[e] += 1; slot_token[j] = t; pos[r, t] = j
    g = np.random.uniform(0.2, 0.8, T)
    w_slot = np.empty(E * C); w_slot[pos[0]] = g; w_slot[pos[1]] = 1.0 - g
    x = pack_weight(n((K, T)) * s[:, None], "e4m3")
    dy = pack_weight(n((N, T)) * v[:, None], "e4m3")
    m1 = n((E, K, H))
    w1 = [pack_weight(m, "e2m1") for m in m1 / np.sqrt(K) / s[None, :, None]]
    w2t = [pack_weight(m, "e2m1") for m in n((E, N, H)) / np.sqrt(N) / v[None, :, None] * u]
    w1t = [pack_weight(m, "e2m1") for m in m1.transpose(0, 2, 1) / np.sqrt(H) / u[None, :, None]]
    return {
        "x_words": x[0],
        "x_scales": x[1],
        "dy_words": dy[0],
        "dy_scales": dy[1],
        "w1_words": np.stack([m[0] for m in w1]),
        "w1_scales": np.stack([m[1] for m in w1]),
        "w2t_words": np.stack([m[0] for m in w2t]),
        "w2t_scales": np.stack([m[1] for m in w2t]),
        "w1t_words": np.stack([m[0] for m in w1t]),
        "w1t_scales": np.stack([m[1] for m in w1t]),
        "gate": (np.tile(w_slot, (128, 1))).astype(np.float32),
        "offs": striped(slot_token),
        "pos1": striped(pos[0]),
        "pos2": striped(pos[1]),
    }


def reference(x_words, x_scales, dy_words, dy_scales, w1_words, w1_scales, w2t_words, w2t_scales, w1t_words, w1t_scales, gate, offs, pos1, pos2):
    w1 = np.stack([unpack_weight(w1_words[e], w1_scales[e], "e2m1") for e in range(E)])
    w2t = np.stack([unpack_weight(w2t_words[e], w2t_scales[e], "e2m1") for e in range(E)])
    w1t = np.stack([unpack_weight(w1t_words[e], w1t_scales[e], "e2m1") for e in range(E)])
    idx = unstriped(offs)
    xq = unpack_weight(x_words, x_scales, "e4m3")[:, idx]
    gq = unpack_weight(dy_words, dy_scales, "e4m3")[:, idx]
    dh = f64(gate[:1]) * by_expert(w2t, gq)
    a = by_expert(w1, xq)
    dx = by_expert(w1t, mxq(dh * d_relu2(a), 0, "e4m3"))
    out = dx[:, unstriped(pos1)] + dx[:, unstriped(pos2)]
    return out

@@ -1,0 +1,253 @@
+from contextlib import ExitStack
+
+import concourse.mybir as mybir
+from concourse.masks import make_identity
+
+K, T, E, C, H, N = 512, 512, 8, 128, 512, 1024
+S = E * C
+P = 128
+FLOPS = 2 * S * (K * H + N * H + H * K)
+
+F32 = mybir.dt.float32
+BF16 = mybir.dt.bfloat16
+I32 = mybir.dt.int32
+U32 = mybir.dt.uint32
+U16 = mybir.dt.uint16
+U8 = mybir.dt.uint8
+FP8X4 = mybir.dt.float8_e4m3fn_x4
+FP4X4 = mybir.dt.float4_e2m1fn_x4
+MULT = mybir.AluOpType.mult
+ADD = mybir.AluOpType.add
+ACT = mybir.ActivationFunctionType
+
+
+def tile_moe_rec_mlp_relu2_kernel(
+    tc, x_words, x_scales, dy_words, dy_scales, w1_words, w1_scales, w2t_words, w2t_scales,
+    w1t_words, w1t_scales, gate, offs, pos1, pos2, out,
+):
+    nc = tc.nc
+    with ExitStack() as ctx:
+        keep = ctx.enter_context(tc.tile_pool(name="keep", bufs=1))
+        psum = ctx.enter_context(tc.psum_pool(name="psum", bufs=1))
+
+        def held(shape, dtype, name):
+            return keep.tile(shape, dtype, name=name, align_bytes=64)
+
+        banks = [psum.tile([P, 512], F32, name="bank%d" % b) for b in range(8)]
+
+        offs_t = held([P, S // 16], U16, "offs_t")
+        pos1_t = held([P, T // 16], U16, "pos1_t")
+        pos2_t = held([P, T // 16], U16, "pos2_t")
+        xw_win = held([P, T], I32, "xw_win")
+        xs_win = held([P, T], U8, "xs_win")
+        dw_win = held([P, 2, T], I32, "dw_win")
+        ds_win = held([P, T], U8, "ds_win")
+        xw = held([P, S], U32, "xw")
+        xs = held([P, S], U8, "xs")
+        dw = [held([P, S], U32, "dw%d" % s) for s in range(2)]
+        ds0 = held([P, S], U8, "ds0")
+        ds1 = held([P, S], U8, "ds1")
+        gate_rows = held([P, C], F32, "gate_rows")
+        gate2 = held([P, E], F32, "gate2")
+        ident = held([P, P], F32, "ident")
+        w1 = [held([P, 4, 2 * H], U8, "w1_%d" % h) for h in range(2)]
+        w2 = [held([P, 4, 2 * H], U8, "w2_%d" % h) for h in range(4)]
+        w1t = [held([P, 4, 2 * K], U8, "w1t_%d" % h) for h in range(2)]
+        w1s = held([P, E, H], U8, "w1s")
+        w2s = held([P, 2 * E, H], U8, "w2s")
+        w1ts = held([P, E, K], U8, "w1ts")
+        relu_a = [held([P, H], F32, "relu_a%d" % e) for e in range(E)]
+        da = [held([P, H], BF16, "da%d" % e) for e in range(E)]
+        groups = [(0, 1), (2, 3), (4, 5), (6,), (7,)]
+        da_t = [held([P, len(g) * C * 4], BF16, "da_t%d" % g[0]) for g in groups]
+        da_codes = [held([P, len(g) * C], U32, "da_codes%d" % g[0]) for g in groups]
+        da_scales = [held([P, len(g) * C], U8, "da_scales%d" % g[0]) for g in groups]
+        dx = held([P, 4, S], F32, "dx")
+
+        def zero(engine, plane):
+            engine.memset(plane.bitcast(I32), 0)
+
+        zero(nc.vector, ds_win[:])
+        zero(nc.vector, xs_win[:])
+        zero(nc.vector, w1s[:].rearrange("p e n -> p (e n)"))
+        zero(nc.vector, w2s[:].rearrange("p e n -> p (e n)"))
+        zero(nc.vector, ds1[:])
+        zero(nc.gpsimd, w1ts[:].rearrange("p e n -> p (e n)"))
+        make_identity(nc, ident[:])
+
+        def load_scales(plane, rows):
+            by_row = rows.rearrange("e s (q r) n -> r q (e s) n", r=4)
+            for r in range(4):
+                nc.sync.dma_start(plane[r:P:32, :, :].bitcast(I32), by_row[r].bitcast(I32))
+
+        def load_words(tile, words):
+            nc.sync.dma_start(tile[:].bitcast(I32), words.rearrange("e s p b -> p (e s) b").bitcast(I32))
+
+        nc.sync.dma_start(offs_t[:], offs)
+        for q in range(4):
+            nc.sync.dma_start(ds_win[32 * q : 32 * q + 8, :].bitcast(I32), dy_scales[:, 4 * q : 4 * q + 4, :].bitcast(I32))
+        nc.sync.dma_start(xw_win[:], x_words[0].rearrange("p t d -> p (t d)").bitcast(I32))
+        for q in range(4):
+            nc.sync.dma_start(xs_win[32 * q : 32 * q + 4, :].bitcast(I32), x_scales[0, 4 * q : 4 * q + 4, :].bitcast(I32))
+        nc.sync.dma_start(dw_win[:], dy_words.rearrange("s p t d -> p s (t d)").bitcast(I32))
+        nc.sync.dma_start(gate_rows[:], gate[0:16, :].rearrange("r (e c) -> (r e) c", c=C))
+        load_scales(w1s, w1_scales)
+        load_words(w1[0], w1_words[0:4])
+        load_words(w1[1], w1_words[4:8])
+        load_scales(w2s, w2t_scales)
+        load_words(w2[0], w2t_words[0:2])
+        load_words(w2[1], w2t_words[2:4])
+        load_scales(w1ts, w1t_scales)
+        load_words(w1t[0], w1t_words[0:4])
+        load_words(w2[2], w2t_words[4:6])
+        load_words(w2[3], w2t_words[6:8])
+        load_words(w1t[1], w1t_words[4:8])
+        nc.sync.dma_start(pos1_t[:], pos1)
+        nc.sync.dma_start(pos2_t[:], pos2)
+
+        def gather(dst, window, lo, hi):
+            nc.vector.tensor_copy(dst[:, lo:hi], window.indirect(offs_t[:, lo // 16 : hi // 16]))
+
+        cuts = [(0, 384), (384, 768), (768, 1024)]
+        for lo, hi in cuts:
+            gather(ds0, ds_win[:], lo, hi)
+        nc.gpsimd.dma_start(ds1[0:100, :].bitcast(I32), ds0[4:104, :].bitcast(I32))
+
+        nc.tensor.transpose(banks[6][:, 0:P], gate_rows[:], ident[:])
+        nc.scalar.activation(gate2[:], banks[6][:, 0:E], ACT.Copy, scale=2.0)
+
+        def slots(e):
+            return slice(e * C, (e + 1) * C)
+
+        for lo, hi in cuts:
+            gather(xw, xw_win[:].bitcast(U32), lo, hi)
+            gather(xs, xs_win[:], lo, hi)
+            for e in range(lo // C, hi // C):
+                bank = banks[e % 2]
+                nc.tensor.matmul_mx(
+                    bank[:], lhsT=xw[:, slots(e)].bitcast(FP8X4), lhsT_scale=xs[:, slots(e)],
+                    rhs=w1[e // 4][:, e % 4, :].bitcast(FP4X4), rhs_scale=w1s[:, e, :], start=True, stop=True,
+                )
+                nc.scalar.activation(relu_a[e][:], bank[:], ACT.Relu)
+
+        def dh_bank(e):
+            return banks[2 + e % 4]
+
+        def gather_dy(pair):
+            for s in range(2):
+                gather(dw[s], dw_win[:, s, :].bitcast(U32), 256 * pair, 256 * (pair + 1))
+
+        def make_dh(e):
+            for s, plane in enumerate((ds0, ds1)):
+                nc.tensor.matmul_mx(
+                    dh_bank(e)[:], lhsT=dw[s][:, slots(e)].bitcast(FP8X4), lhsT_scale=plane[:, slots(e)],
+                    rhs=w2[e // 2][:, 2 * (e % 2) + s, :].bitcast(FP4X4), rhs_scale=w2s[:, 2 * e + s, :],
+                    start=(s == 0), stop=(s == 1),
+                )
+
+        def make_da(e):
+            nc.vector.scalar_tensor_tensor(da[e][:], dh_bank(e)[:], gate2[:, e : e + 1], relu_a[e][:], MULT, MULT)
+
+        def turn(g):
+            members = groups[g]
+            bank = banks[6 + g % 2]
+            for m, e in enumerate(members):
+                words = da[e][:].bitcast(F32)
+                for u in range(2):
+                    nc.tensor.transpose(bank[:, (2 * m + u) * C : (2 * m + u + 1) * C], words[:, u : 2 * P : 2], ident[:])
+            width = len(members) * 2 * C
+            nc.scalar.copy(
+                da_t[g][:].bitcast(F32).rearrange("p (m c u) -> p m c u", c=C, u=2),
+                bank[:, 0:width].rearrange("p (m u c) -> p m c u", c=C, u=2),
+            )
+
+        def quantize(g):
+            nc.vector.quantize_mx(da_codes[g][:].bitcast(FP8X4), da_scales[g][:], da_t[g][:])
+
+        def make_dx(g):
+            for m, e in enumerate(groups[g]):
+                last = e == E - 1
+                for kt in range(4):
+                    bank = banks[2] if last and kt == 0 else banks[e % 2]
+                    nc.tensor.matmul_mx(
+                        bank[:, kt * C : (kt + 1) * C],
+                        lhsT=w1t[e // 4][:, e % 4, 2 * kt * P : 2 * (kt + 1) * P].bitcast(FP4X4),
+                        lhsT_scale=w1ts[:, e, kt * P : (kt + 1) * P],
+                        rhs=da_codes[g][:, m * C : (m + 1) * C].bitcast(FP8X4),
+                        rhs_scale=da_scales[g][:, m * C : (m + 1) * C], start=True, stop=True,
+                    )
+                    if last and kt == 0:
+                        nc.scalar.copy(dx[:, 0, slots(e)], bank[:, 0:C])
+                first = 1 if last else 0
+                nc.scalar.copy(dx[:, first:4, slots(e)], banks[e % 2][:, first * C :].rearrange("p (k c) -> p k c", c=C))
+
+        gather_dy(0)
+        make_dh(0)
+        make_dh(1)
+        gather_dy(1)
+        make_dh(2)
+        make_dh(3)
+        gather_dy(2)
+        make_da(0)
+        make_da(1)
+        turn(0)
+        make_dh(4)
+        make_dh(5)
+        make_da(2)
+        make_da(3)
+        quantize(0)
+        turn(1)
+        make_dx(0)
+        gather_dy(3)
+        make_dh(6)
+        make_dh(7)
+        quantize(1)
+        make_dx(1)
+        make_da(4)
+        make_da(5)
+        turn(2)
+        make_da(6)
+        turn(3)
+        quantize(2)
+        make_da(7)
+        turn(4)
+        make_dx(2)
+        quantize(3)
+        make_dx(3)
+        quantize(4)
+        make_dx(4)
+
+        first_pick = [held([P, T], F32, "first_pick%d" % kt) for kt in range(4)]
+        second_pick = [held([P, T], F32, "second_pick%d" % kt) for kt in range(4)]
+        turned_sum = [held([P, T], F32, "turned_sum%d" % kt) for kt in range(3)]
+        total = [held([P, T], F32, "total%d" % kt) for kt in range(4)]
+
+        def pick(dst, kt, pos_t, lo, hi):
+            nc.vector.tensor_copy(dst[:, lo:hi], dx[:, kt, :].indirect(pos_t[:, lo // 16 : hi // 16]))
+
+        for kt in range(3):
+            pick(first_pick[kt], kt, pos1_t, 0, T)
+            pick(second_pick[kt], kt, pos2_t, 0, T)
+            sum_bank, back_bank = banks[3 + kt % 2], banks[5 + kt % 2]
+            for b in range(4):
+                block = slice(b * P, (b + 1) * P)
+                nc.tensor.matmul(sum_bank[:, block], first_pick[kt][:, block], ident[:], start=True, stop=False, is_transpose=True)
+                nc.tensor.matmul(sum_bank[:, block], second_pick[kt][:, block], ident[:], start=False, stop=True, is_transpose=True)
+            nc.scalar.copy(turned_sum[kt][:], sum_bank[:])
+            for b in range(4):
+                block = slice(b * P, (b + 1) * P)
+                nc.tensor.transpose(back_bank[:, block], turned_sum[kt][:, block], ident[:])
+            nc.scalar.copy(total[kt][:], back_bank[:])
+            nc.sync.dma_start(out[kt * P : (kt + 1) * P, :], total[kt][:])
+
+        def finish(lo, hi):
+            nc.vector.tensor_tensor(total[3][:, lo:hi], first_pick[3][:, lo:hi], second_pick[3][:, lo:hi], ADD)
+            nc.sync.dma_start(out[3 * P :, lo:hi], total[3][:, lo:hi])
+
+        half = T // 2
+        pick(first_pick[3], 3, pos1_t, 0, half)
+        pick(second_pick[3], 3, pos2_t, 0, half)
+        pick(first_pick[3], 3, pos1_t, half, T)
+        finish(0, half)
+        pick(second_pick[3], 3, pos2_t, half, T)
+        finish(half, T)

@@ -50,7 +50,7 @@ def tile_moe_rec_mlp_relu2_kernel(
         gate_rows = held([P, C], F32, "gate_rows")
         gate2 = held([P, E], F32, "gate2")
         ident = held([P, P], F32, "ident")
-        w1 = [held([P, 4, 2 * H], U8, "w1_%d" % h) for h in range(2)]
+        w1 = held([P, E, 2 * H], U8, "w1")
         w2 = [held([P, 4, 2 * H], U8, "w2_%d" % h) for h in range(4)]
         w1t = [held([P, 4, 2 * K], U8, "w1t_%d" % h) for h in range(2)]
         w1s = held([P, E, H], U8, "w1s")
@@ -67,13 +67,13 @@ def tile_moe_rec_mlp_relu2_kernel(
         def zero(engine, plane):
             engine.memset(plane.bitcast(I32), 0)
 
-        zero(nc.vector, ds_win[:])
-        zero(nc.vector, xs_win[:])
+        zero(nc.gpsimd, ds_win[:])
+        zero(nc.gpsimd, xs_win[:])
         zero(nc.vector, w1s[:].rearrange("p e n -> p (e n)"))
         zero(nc.vector, w2s[:].rearrange("p e n -> p (e n)"))
-        zero(nc.vector, ds1[:])
-        zero(nc.gpsimd, w1ts[:].rearrange("p e n -> p (e n)"))
+        zero(nc.gpsimd, ds1[:])
         make_identity(nc, ident[:])
+        zero(nc.gpsimd, w1ts[:].rearrange("p e n -> p (e n)"))
 
         def load_scales(plane, rows):
             by_row = rows.rearrange("e s (q r) n -> r q (e s) n", r=4)
@@ -87,20 +87,21 @@ def tile_moe_rec_mlp_relu2_kernel(
         for q in range(4):
             nc.sync.dma_start(ds_win[32 * q : 32 * q + 8, :].bitcast(I32), dy_scales[:, 4 * q : 4 * q + 4, :].bitcast(I32))
         nc.sync.dma_start(xw_win[:], x_words[0].rearrange("p t d -> p (t d)").bitcast(I32))
+        load_words(w1[:, 0:4, :], w1_words[0:4])
+        load_words(w1[:, 4:8, :], w1_words[4:8])
         for q in range(4):
             nc.sync.dma_start(xs_win[32 * q : 32 * q + 4, :].bitcast(I32), x_scales[0, 4 * q : 4 * q + 4, :].bitcast(I32))
+        load_scales(w1s, w1_scales)
         nc.sync.dma_start(dw_win[:], dy_words.rearrange("s p t d -> p s (t d)").bitcast(I32))
         nc.sync.dma_start(gate_rows[:], gate[0:16, :].rearrange("r (e c) -> (r e) c", c=C))
-        load_scales(w1s, w1_scales)
-        load_words(w1[0], w1_words[0:4])
-        load_words(w1[1], w1_words[4:8])
         load_scales(w2s, w2t_scales)
         load_words(w2[0], w2t_words[0:2])
         load_words(w2[1], w2t_words[2:4])
         load_scales(w1ts, w1t_scales)
-        load_words(w1t[0], w1t_words[0:4])
         load_words(w2[2], w2t_words[4:6])
-        load_words(w2[3], w2t_words[6:8])
+        load_words(w1t[0], w1t_words[0:4])
+        load_words(w2[3][:, 0:2, :], w2t_words[6:7])
+        load_words(w2[3][:, 2:4, :], w2t_words[7:8])
         load_words(w1t[1], w1t_words[4:8])
         nc.sync.dma_start(pos1_t[:], pos1)
         nc.sync.dma_start(pos2_t[:], pos2)
@@ -121,12 +122,13 @@ def tile_moe_rec_mlp_relu2_kernel(
 
         for lo, hi in cuts:
             gather(xw, xw_win[:].bitcast(U32), lo, hi)
+        for lo, hi in cuts:
             gather(xs, xs_win[:], lo, hi)
             for e in range(lo // C, hi // C):
                 bank = banks[e % 2]
                 nc.tensor.matmul_mx(
                     bank[:], lhsT=xw[:, slots(e)].bitcast(FP8X4), lhsT_scale=xs[:, slots(e)],
-                    rhs=w1[e // 4][:, e % 4, :].bitcast(FP4X4), rhs_scale=w1s[:, e, :], start=True, stop=True,
+                    rhs=w1[:, e, :].bitcast(FP4X4), rhs_scale=w1s[:, e, :], start=True, stop=True,
                 )
                 nc.scalar.activation(relu_a[e][:], bank[:], ACT.Relu)
 
@@ -146,7 +148,14 @@ def tile_moe_rec_mlp_relu2_kernel(
                 )
 
         def make_da(e):
-            nc.vector.scalar_tensor_tensor(da[e][:], dh_bank(e)[:], gate2[:, e : e + 1], relu_a[e][:], MULT, MULT)
+            for u in range(2):
+                nc.vector.scalar_tensor_tensor(
+                    da[e][:, u * 2 * P : (u + 1) * 2 * P].rearrange("c (p d) -> c p d", d=2),
+                    dh_bank(e)[:].rearrange("c (p u d) -> c u p d", u=2, d=2)[:, u],
+                    gate2[:, e : e + 1],
+                    relu_a[e][:].rearrange("c (p u d) -> c u p d", u=2, d=2)[:, u],
+                    MULT, MULT,
+                )
 
         def turn(g):
             members = groups[g]
@@ -154,7 +163,7 @@ def tile_moe_rec_mlp_relu2_kernel(
             for m, e in enumerate(members):
                 words = da[e][:].bitcast(F32)
                 for u in range(2):
-                    nc.tensor.transpose(bank[:, (2 * m + u) * C : (2 * m + u + 1) * C], words[:, u : 2 * P : 2], ident[:])
+                    nc.tensor.transpose(bank[:, (2 * m + u) * C : (2 * m + u + 1) * C], words[:, u * P : (u + 1) * P], ident[:])
             width = len(members) * 2 * C
             nc.scalar.copy(
                 da_t[g][:].bitcast(F32).rearrange("p (m c u) -> p m c u", c=C, u=2),

@@ -6,6 +6,7 @@ from concourse.masks import make_identity
 K, T, E, C, H, N = 512, 512, 8, 128, 512, 1024
 S = E * C
 P = 128
+PAIR = 2 * C
 FLOPS = 2 * S * (K * H + N * H + H * K)
 
 F32 = mybir.dt.float32
@@ -28,12 +29,14 @@ def tile_moe_rec_mlp_relu2_kernel(
     nc = tc.nc
     with ExitStack() as ctx:
         keep = ctx.enter_context(tc.tile_pool(name="keep", bufs=1))
+        ring = ctx.enter_context(tc.tile_pool(name="ring", bufs=2))
         psum = ctx.enter_context(tc.psum_pool(name="psum", bufs=1))
 
         def held(shape, dtype, name):
             return keep.tile(shape, dtype, name=name, align_bytes=64)
 
         banks = [psum.tile([P, 512], F32, name="bank%d" % b) for b in range(8)]
+        a_banks, dh_banks, turn_bank, dx_banks = banks[0:2], banks[2:5], banks[5], banks[6:8]
 
         offs_t = held([P, S // 16], U16, "offs_t")
         pos1_t = held([P, T // 16], U16, "pos1_t")
@@ -42,27 +45,24 @@ def tile_moe_rec_mlp_relu2_kernel(
         xs_win = held([P, T], U8, "xs_win")
         dw_win = held([P, 2, T], I32, "dw_win")
         ds_win = held([P, T], U8, "ds_win")
-        xw = held([P, S], U32, "xw")
-        xs = held([P, S], U8, "xs")
-        dw = [held([P, S], U32, "dw%d" % s) for s in range(2)]
         ds0 = held([P, S], U8, "ds0")
         ds1 = held([P, S], U8, "ds1")
         gate_rows = held([P, C], F32, "gate_rows")
-        gate2 = held([P, E], F32, "gate2")
+        gate_col = held([P, E], F32, "gate_col")
         ident = held([P, P], F32, "ident")
-        w1 = held([P, E, 2 * H], U8, "w1")
+        w1 = [held([P, n, 2 * H], U8, "w1_%d" % h) for h, n in enumerate((2, 2, 4))]
         w2 = [held([P, 4, 2 * H], U8, "w2_%d" % h) for h in range(4)]
         w1t = [held([P, 4, 2 * K], U8, "w1t_%d" % h) for h in range(2)]
         w1s = held([P, E, H], U8, "w1s")
         w2s = held([P, 2 * E, H], U8, "w2s")
         w1ts = held([P, E, K], U8, "w1ts")
-        relu_a = [held([P, H], F32, "relu_a%d" % e) for e in range(E)]
+        slope = [held([P, H], F32, "slope%d" % e) for e in range(E)]
         da = [held([P, H], BF16, "da%d" % e) for e in range(E)]
         groups = [(0, 1), (2, 3), (4, 5), (6,), (7,)]
         da_t = [held([P, len(g) * C * 4], BF16, "da_t%d" % g[0]) for g in groups]
         da_codes = [held([P, len(g) * C], U32, "da_codes%d" % g[0]) for g in groups]
         da_scales = [held([P, len(g) * C], U8, "da_scales%d" % g[0]) for g in groups]
-        dx = held([P, 4, S], F32, "dx")
+        dx = [held([P, S], F32, "dx%d" % kt) for kt in range(4)]
 
         def zero(engine, plane):
             engine.memset(plane.bitcast(I32), 0)
@@ -71,9 +71,10 @@ def tile_moe_rec_mlp_relu2_kernel(
         zero(nc.gpsimd, xs_win[:])
         zero(nc.vector, w1s[:].rearrange("p e n -> p (e n)"))
         zero(nc.vector, w2s[:].rearrange("p e n -> p (e n)"))
+        zero(nc.vector, w1ts[:].rearrange("p e n -> p (e n)"))
+        nc.gpsimd.memset(gate_rows[:], 0.0)
         zero(nc.gpsimd, ds1[:])
         make_identity(nc, ident[:])
-        zero(nc.gpsimd, w1ts[:].rearrange("p e n -> p (e n)"))
 
         def load_scales(plane, rows):
             by_row = rows.rearrange("e s (q r) n -> r q (e s) n", r=4)
@@ -87,79 +88,89 @@ def tile_moe_rec_mlp_relu2_kernel(
         for q in range(4):
             nc.sync.dma_start(ds_win[32 * q : 32 * q + 8, :].bitcast(I32), dy_scales[:, 4 * q : 4 * q + 4, :].bitcast(I32))
         nc.sync.dma_start(xw_win[:], x_words[0].rearrange("p t d -> p (t d)").bitcast(I32))
-        load_words(w1[:, 0:4, :], w1_words[0:4])
-        load_words(w1[:, 4:8, :], w1_words[4:8])
+        nc.sync.dma_start(dw_win[:], dy_words.rearrange("s p t d -> p s (t d)").bitcast(I32))
+        load_words(w1[0], w1_words[0:2])
         for q in range(4):
             nc.sync.dma_start(xs_win[32 * q : 32 * q + 4, :].bitcast(I32), x_scales[0, 4 * q : 4 * q + 4, :].bitcast(I32))
         load_scales(w1s, w1_scales)
-        nc.sync.dma_start(dw_win[:], dy_words.rearrange("s p t d -> p s (t d)").bitcast(I32))
-        nc.sync.dma_start(gate_rows[:], gate[0:16, :].rearrange("r (e c) -> (r e) c", c=C))
-        load_scales(w2s, w2t_scales)
         load_words(w2[0], w2t_words[0:2])
+        load_words(w1[1], w1_words[2:4])
+        load_scales(w2s, w2t_scales)
+        nc.sync.dma_start(gate_rows[0:E, :], gate[0, :].rearrange("(e c) -> e c", c=C))
         load_words(w2[1], w2t_words[2:4])
-        load_scales(w1ts, w1t_scales)
+        load_words(w1[2], w1_words[4:8])
         load_words(w2[2], w2t_words[4:6])
+        load_scales(w1ts, w1t_scales)
         load_words(w1t[0], w1t_words[0:4])
-        load_words(w2[3][:, 0:2, :], w2t_words[6:7])
-        load_words(w2[3][:, 2:4, :], w2t_words[7:8])
+        load_words(w2[3], w2t_words[6:8])
         load_words(w1t[1], w1t_words[4:8])
         nc.sync.dma_start(pos1_t[:], pos1)
         nc.sync.dma_start(pos2_t[:], pos2)
 
         def gather(dst, window, lo, hi):
-            nc.vector.tensor_copy(dst[:, lo:hi], window.indirect(offs_t[:, lo // 16 : hi // 16]))
+            nc.vector.tensor_copy(dst, window.indirect(offs_t[:, lo // 16 : hi // 16]))
 
-        cuts = [(0, 384), (384, 768), (768, 1024)]
-        for lo, hi in cuts:
-            gather(ds0, ds_win[:], lo, hi)
-        nc.gpsimd.dma_start(ds1[0:100, :].bitcast(I32), ds0[4:104, :].bitcast(I32))
+        for lo, hi in [(0, 384), (384, 768), (768, 1024)]:
+            gather(ds0[:, lo:hi], ds_win[:], lo, hi)
+        nc.scalar.dma_start(ds1[0:100, :].bitcast(I32), ds0[4:104, :].bitcast(I32))
 
-        nc.tensor.transpose(banks[6][:, 0:P], gate_rows[:], ident[:])
-        nc.scalar.activation(gate2[:], banks[6][:, 0:E], ACT.Copy, scale=2.0)
+        nc.tensor.transpose(turn_bank[:, 0:P], gate_rows[:], ident[:])
+        nc.scalar.copy(gate_col[:], turn_bank[:, 0:E])
 
         def slots(e):
             return slice(e * C, (e + 1) * C)
 
-        for lo, hi in cuts:
-            gather(xw, xw_win[:].bitcast(U32), lo, hi)
-        for lo, hi in cuts:
-            gather(xs, xs_win[:], lo, hi)
-            for e in range(lo // C, hi // C):
-                bank = banks[e % 2]
-                nc.tensor.matmul_mx(
-                    bank[:], lhsT=xw[:, slots(e)].bitcast(FP8X4), lhsT_scale=xs[:, slots(e)],
-                    rhs=w1[:, e, :].bitcast(FP4X4), rhs_scale=w1s[:, e, :], start=True, stop=True,
-                )
-                nc.scalar.activation(relu_a[e][:], bank[:], ACT.Relu)
+        def w1_of(e):
+            return w1[e // 2][:, e % 2, :] if e < 4 else w1[2][:, e - 4, :]
 
         def dh_bank(e):
-            return banks[2 + e % 4]
+            return dh_banks[e % 3]
+
+        def forward(pair):
+            lo, hi = PAIR * pair, PAIR * (pair + 1)
+            xw = ring.tile([P, PAIR], U32, name="xw", align_bytes=64)
+            xs = ring.tile([P, PAIR], U8, name="xs", align_bytes=64)
+            gather(xw[:], xw_win[:].bitcast(U32), lo, hi)
+            gather(xs[:], xs_win[:], lo, hi)
+            for m in range(2):
+                e = 2 * pair + m
+                nc.tensor.matmul_mx(
+                    a_banks[m][:], lhsT=xw[:, slots(m)].bitcast(FP8X4), lhsT_scale=xs[:, slots(m)],
+                    rhs=w1_of(e).bitcast(FP4X4), rhs_scale=w1s[:, e, :], start=True, stop=True,
+                )
+                nc.scalar.activation(
+                    slope[e][:].rearrange("c (u p d) -> c u p d", u=2, d=2),
+                    a_banks[m][:].rearrange("c (p u d) -> c u p d", u=2, d=2),
+                    ACT.Relu, scale=2.0,
+                )
 
         def gather_dy(pair):
+            dw = [ring.tile([P, PAIR], U32, name="dw%d" % s, align_bytes=64) for s in range(2)]
             for s in range(2):
-                gather(dw[s], dw_win[:, s, :].bitcast(U32), 256 * pair, 256 * (pair + 1))
+                gather(dw[s][:], dw_win[:, s, :].bitcast(U32), PAIR * pair, PAIR * (pair + 1))
+            return dw
 
-        def make_dh(e):
+        def make_dh(e, dw):
             for s, plane in enumerate((ds0, ds1)):
                 nc.tensor.matmul_mx(
-                    dh_bank(e)[:], lhsT=dw[s][:, slots(e)].bitcast(FP8X4), lhsT_scale=plane[:, slots(e)],
+                    dh_bank(e)[:], lhsT=dw[s][:, slots(e % 2)].bitcast(FP8X4), lhsT_scale=plane[:, slots(e)],
                     rhs=w2[e // 2][:, 2 * (e % 2) + s, :].bitcast(FP4X4), rhs_scale=w2s[:, 2 * e + s, :],
                     start=(s == 0), stop=(s == 1),
                 )
 
         def make_da(e):
             for u in range(2):
+                half = slice(u * 2 * P, (u + 1) * 2 * P)
                 nc.vector.scalar_tensor_tensor(
-                    da[e][:, u * 2 * P : (u + 1) * 2 * P].rearrange("c (p d) -> c p d", d=2),
+                    da[e][:, half].rearrange("c (p d) -> c p d", d=2),
                     dh_bank(e)[:].rearrange("c (p u d) -> c u p d", u=2, d=2)[:, u],
-                    gate2[:, e : e + 1],
-                    relu_a[e][:].rearrange("c (p u d) -> c u p d", u=2, d=2)[:, u],
+                    gate_col[:, e : e + 1],
+                    slope[e][:, half].rearrange("c (p d) -> c p d", d=2),
                     MULT, MULT,
                 )
 
-        def turn(g):
+        def turn(g, bank):
             members = groups[g]
-            bank = banks[6 + g % 2]
             for m, e in enumerate(members):
                 words = da[e][:].bitcast(F32)
                 for u in range(2):
@@ -173,90 +184,89 @@ def tile_moe_rec_mlp_relu2_kernel(
         def quantize(g):
             nc.vector.quantize_mx(da_codes[g][:].bitcast(FP8X4), da_scales[g][:], da_t[g][:])
 
-        def make_dx(g):
-            for m, e in enumerate(groups[g]):
-                last = e == E - 1
-                for kt in range(4):
-                    bank = banks[2] if last and kt == 0 else banks[e % 2]
-                    nc.tensor.matmul_mx(
-                        bank[:, kt * C : (kt + 1) * C],
-                        lhsT=w1t[e // 4][:, e % 4, 2 * kt * P : 2 * (kt + 1) * P].bitcast(FP4X4),
-                        lhsT_scale=w1ts[:, e, kt * P : (kt + 1) * P],
-                        rhs=da_codes[g][:, m * C : (m + 1) * C].bitcast(FP8X4),
-                        rhs_scale=da_scales[g][:, m * C : (m + 1) * C], start=True, stop=True,
-                    )
-                    if last and kt == 0:
-                        nc.scalar.copy(dx[:, 0, slots(e)], bank[:, 0:C])
-                first = 1 if last else 0
-                nc.scalar.copy(dx[:, first:4, slots(e)], banks[e % 2][:, first * C :].rearrange("p (k c) -> p k c", c=C))
+        def dx_product(g, m, kt, dst):
+            e = groups[g][m]
+            nc.tensor.matmul_mx(
+                dst,
+                lhsT=w1t[e // 4][:, e % 4, 2 * kt * P : 2 * (kt + 1) * P].bitcast(FP4X4),
+                lhsT_scale=w1ts[:, e, kt * P : (kt + 1) * P],
+                rhs=da_codes[g][:, slots(m)].bitcast(FP8X4),
+                rhs_scale=da_scales[g][:, slots(m)], start=True, stop=True,
+            )
 
-        gather_dy(0)
-        make_dh(0)
-        make_dh(1)
-        gather_dy(1)
-        make_dh(2)
-        make_dh(3)
-        gather_dy(2)
+        def make_dx(g):
+            for kt in range(4):
+                dst = dx_banks[kt // 2][:, (kt % 2) * PAIR : (kt % 2 + 1) * PAIR]
+                for m in range(2):
+                    dx_product(g, m, kt, dst[:, slots(m)])
+            for kt in range(4):
+                nc.scalar.copy(dx[kt][:, g * PAIR : (g + 1) * PAIR], dx_banks[kt // 2][:, (kt % 2) * PAIR : (kt % 2 + 1) * PAIR])
+
+        forward(0)
+        dw = gather_dy(0)
+        make_dh(0, dw)
+        make_dh(1, dw)
+        forward(1)
+        dw = gather_dy(1)
+        make_dh(2, dw)
         make_da(0)
+        make_dh(3, dw)
         make_da(1)
-        turn(0)
-        make_dh(4)
-        make_dh(5)
-        make_da(2)
-        make_da(3)
+        turn(0, turn_bank)
+        forward(2)
+        dw = gather_dy(2)
+        make_dh(4, dw)
         quantize(0)
-        turn(1)
         make_dx(0)
-        gather_dy(3)
-        make_dh(6)
-        make_dh(7)
+        make_da(2)
+        make_dh(5, dw)
+        make_da(3)
+        turn(1, turn_bank)
+        forward(3)
+        dw = gather_dy(3)
+        make_dh(6, dw)
         quantize(1)
-        make_dx(1)
         make_da(4)
+        make_dh(7, dw)
+        make_dx(1)
         make_da(5)
-        turn(2)
+        turn(2, turn_bank)
         make_da(6)
-        turn(3)
-        quantize(2)
+        turn(3, a_banks[0])
         make_da(7)
-        turn(4)
-        make_dx(2)
+        turn(4, a_banks[1])
+
+        late = [(2, 0), (2, 1), (3, 0), (4, 0)]
+        late_banks = [dx_banks[0], dx_banks[1], dh_bank(6), dh_bank(7)]
+        quantize(2)
+        dx_product(2, 0, 0, late_banks[0][:, slots(0)])
+        dx_product(2, 1, 0, late_banks[0][:, slots(1)])
         quantize(3)
-        make_dx(3)
+        dx_product(3, 0, 0, late_banks[0][:, slots(2)])
+        nc.scalar.copy(dx[0][:, 4 * C : 7 * C], late_banks[0][:, 0 : 3 * C])
         quantize(4)
-        make_dx(4)
+        dx_product(4, 0, 0, dh_bank(5)[:, 0:C])
+        nc.scalar.copy(dx[0][:, 7 * C :], dh_bank(5)[:, 0:C])
+        for kt in range(1, 4):
+            for j, (g, m) in enumerate(late):
+                dx_product(g, m, kt, late_banks[kt][:, slots(j)])
+            nc.scalar.copy(dx[kt][:, 4 * C :], late_banks[kt][:])
 
         first_pick = [held([P, T], F32, "first_pick%d" % kt) for kt in range(4)]
-        second_pick = [held([P, T], F32, "second_pick%d" % kt) for kt in range(4)]
-        turned_sum = [held([P, T], F32, "turned_sum%d" % kt) for kt in range(3)]
         total = [held([P, T], F32, "total%d" % kt) for kt in range(4)]
 
-        def pick(dst, kt, pos_t, lo, hi):
-            nc.vector.tensor_copy(dst[:, lo:hi], dx[:, kt, :].indirect(pos_t[:, lo // 16 : hi // 16]))
+        def pick(kt):
+            nc.vector.tensor_copy(first_pick[kt][:], dx[kt][:].indirect(pos1_t[:]))
 
+        def finish(kt, lo, hi):
+            nc.vector.tensor_tensor(
+                total[kt][:, lo:hi], dx[kt][:].indirect(pos2_t[:, lo // 16 : hi // 16]), first_pick[kt][:, lo:hi], ADD
+            )
+            nc.sync.dma_start(out[kt * P : (kt + 1) * P, lo:hi], total[kt][:, lo:hi])
+
+        pick(0)
         for kt in range(3):
-            pick(first_pick[kt], kt, pos1_t, 0, T)
-            pick(second_pick[kt], kt, pos2_t, 0, T)
-            sum_bank, back_bank = banks[3 + kt % 2], banks[5 + kt % 2]
-            for b in range(4):
-                block = slice(b * P, (b + 1) * P)
-                nc.tensor.matmul(sum_bank[:, block], first_pick[kt][:, block], ident[:], start=True, stop=False, is_transpose=True)
-                nc.tensor.matmul(sum_bank[:, block], second_pick[kt][:, block], ident[:], start=False, stop=True, is_transpose=True)
-            nc.scalar.copy(turned_sum[kt][:], sum_bank[:])
-            for b in range(4):
-                block = slice(b * P, (b + 1) * P)
-                nc.tensor.transpose(back_bank[:, block], turned_sum[kt][:, block], ident[:])
-            nc.scalar.copy(total[kt][:], back_bank[:])
-            nc.sync.dma_start(out[kt * P : (kt + 1) * P, :], total[kt][:])
-
-        def finish(lo, hi):
-            nc.vector.tensor_tensor(total[3][:, lo:hi], first_pick[3][:, lo:hi], second_pick[3][:, lo:hi], ADD)
-            nc.sync.dma_start(out[3 * P :, lo:hi], total[3][:, lo:hi])
-
-        half = T // 2
-        pick(first_pick[3], 3, pos1_t, 0, half)
-        pick(second_pick[3], 3, pos2_t, 0, half)
-        pick(first_pick[3], 3, pos1_t, half, T)
-        finish(0, half)
-        pick(second_pick[3], 3, pos2_t, half, T)
-        finish(half, T)
+            pick(kt + 1)
+            finish(kt, 0, T)
+        finish(3, 0, T // 2)
+        finish(3, T // 2, T)

@@ -29,14 +29,12 @@ def tile_moe_rec_mlp_relu2_kernel(
     nc = tc.nc
     with ExitStack() as ctx:
         keep = ctx.enter_context(tc.tile_pool(name="keep", bufs=1))
-        ring = ctx.enter_context(tc.tile_pool(name="ring", bufs=2))
         psum = ctx.enter_context(tc.psum_pool(name="psum", bufs=1))
 
-        def held(shape, dtype, name):
-            return keep.tile(shape, dtype, name=name, align_bytes=64)
+        def held(shape, dtype, name, tag=None):
+            return keep.tile(shape, dtype, name=name, tag=tag or name, align_bytes=64)
 
         banks = [psum.tile([P, 512], F32, name="bank%d" % b) for b in range(8)]
-        a_banks, dh_banks, turn_bank, dx_banks = banks[0:2], banks[2:5], banks[5], banks[6:8]
 
         offs_t = held([P, S // 16], U16, "offs_t")
         pos1_t = held([P, T // 16], U16, "pos1_t")
@@ -44,21 +42,23 @@ def tile_moe_rec_mlp_relu2_kernel(
         xw_win = held([P, T], I32, "xw_win")
         xs_win = held([P, T], U8, "xs_win")
         dw_win = held([P, 2, T], I32, "dw_win")
-        ds_win = held([P, T], U8, "ds_win")
+        ds_win = held([P, T], U8, "ds_win", tag="ds_win_then_w1ts")
+        xw = held([P, S], U32, "xw")
+        xs = held([P, S], U8, "xs")
+        dw = [held([P, S], U32, "dw%d" % s) for s in range(2)]
         ds0 = held([P, S], U8, "ds0")
         ds1 = held([P, S], U8, "ds1")
         gate_rows = held([P, C], F32, "gate_rows")
         gate_col = held([P, E], F32, "gate_col")
         ident = held([P, P], F32, "ident")
-        w1 = [held([P, n, 2 * H], U8, "w1_%d" % h) for h, n in enumerate((2, 2, 4))]
+        w1 = [held([P, 4, 2 * H], U8, "w1_%d" % h) for h in range(2)]
         w2 = [held([P, 4, 2 * H], U8, "w2_%d" % h) for h in range(4)]
         w1t = [held([P, 4, 2 * K], U8, "w1t_%d" % h) for h in range(2)]
         w1s = held([P, E, H], U8, "w1s")
         w2s = held([P, 2 * E, H], U8, "w2s")
-        w1ts = held([P, E, K], U8, "w1ts")
         slope = [held([P, H], F32, "slope%d" % e) for e in range(E)]
         da = [held([P, H], BF16, "da%d" % e) for e in range(E)]
-        groups = [(0, 1), (2, 3), (4, 5), (6,), (7,)]
+        groups = [(0, 1, 2, 3), (4, 5), (6,), (7,)]
         da_t = [held([P, len(g) * C * 4], BF16, "da_t%d" % g[0]) for g in groups]
         da_codes = [held([P, len(g) * C], U32, "da_codes%d" % g[0]) for g in groups]
         da_scales = [held([P, len(g) * C], U8, "da_scales%d" % g[0]) for g in groups]
@@ -71,7 +71,6 @@ def tile_moe_rec_mlp_relu2_kernel(
         zero(nc.gpsimd, xs_win[:])
         zero(nc.vector, w1s[:].rearrange("p e n -> p (e n)"))
         zero(nc.vector, w2s[:].rearrange("p e n -> p (e n)"))
-        zero(nc.vector, w1ts[:].rearrange("p e n -> p (e n)"))
         nc.gpsimd.memset(gate_rows[:], 0.0)
         zero(nc.gpsimd, ds1[:])
         make_identity(nc, ident[:])
@@ -88,75 +87,68 @@ def tile_moe_rec_mlp_relu2_kernel(
         for q in range(4):
             nc.sync.dma_start(ds_win[32 * q : 32 * q + 8, :].bitcast(I32), dy_scales[:, 4 * q : 4 * q + 4, :].bitcast(I32))
         nc.sync.dma_start(xw_win[:], x_words[0].rearrange("p t d -> p (t d)").bitcast(I32))
-        nc.sync.dma_start(dw_win[:], dy_words.rearrange("s p t d -> p s (t d)").bitcast(I32))
-        load_words(w1[0], w1_words[0:2])
+        load_words(w1[0], w1_words[0:4])
+        load_words(w1[1], w1_words[4:8])
         for q in range(4):
             nc.sync.dma_start(xs_win[32 * q : 32 * q + 4, :].bitcast(I32), x_scales[0, 4 * q : 4 * q + 4, :].bitcast(I32))
         load_scales(w1s, w1_scales)
+        nc.sync.dma_start(dw_win[:], dy_words.rearrange("s p t d -> p s (t d)").bitcast(I32))
         load_words(w2[0], w2t_words[0:2])
-        load_words(w1[1], w1_words[2:4])
-        load_scales(w2s, w2t_scales)
         nc.sync.dma_start(gate_rows[0:E, :], gate[0, :].rearrange("(e c) -> e c", c=C))
-        load_words(w2[1], w2t_words[2:4])
-        load_words(w1[2], w1_words[4:8])
-        load_words(w2[2], w2t_words[4:6])
+        load_scales(w2s, w2t_scales)
+        for pair in range(1, 4):
+            load_words(w2[pair], w2t_words[2 * pair : 2 * pair + 2])
+
+        def gather(dst, window, lo, hi):
+            nc.vector.tensor_copy(dst[:, lo:hi], window.indirect(offs_t[:, lo // 16 : hi // 16]))
+
+        cuts = [(0, 384), (384, 768), (768, 1024)]
+        for lo, hi in cuts:
+            gather(ds0, ds_win[:], lo, hi)
+        nc.gpsimd.dma_start(ds1[0:100, :].bitcast(I32), ds0[4:104, :].bitcast(I32))
+
+        w1ts = held([P, E, K], U8, "w1ts", tag="ds_win_then_w1ts")
+        zero(nc.gpsimd, w1ts[:].rearrange("p e n -> p (e n)"))
         load_scales(w1ts, w1t_scales)
         load_words(w1t[0], w1t_words[0:4])
-        load_words(w2[3], w2t_words[6:8])
         load_words(w1t[1], w1t_words[4:8])
         nc.sync.dma_start(pos1_t[:], pos1)
         nc.sync.dma_start(pos2_t[:], pos2)
 
-        def gather(dst, window, lo, hi):
-            nc.vector.tensor_copy(dst, window.indirect(offs_t[:, lo // 16 : hi // 16]))
-
-        for lo, hi in [(0, 384), (384, 768), (768, 1024)]:
-            gather(ds0[:, lo:hi], ds_win[:], lo, hi)
-        nc.scalar.dma_start(ds1[0:100, :].bitcast(I32), ds0[4:104, :].bitcast(I32))
-
-        nc.tensor.transpose(turn_bank[:, 0:P], gate_rows[:], ident[:])
-        nc.scalar.copy(gate_col[:], turn_bank[:, 0:E])
-
         def slots(e):
             return slice(e * C, (e + 1) * C)
 
-        def w1_of(e):
-            return w1[e // 2][:, e % 2, :] if e < 4 else w1[2][:, e - 4, :]
-
-        def dh_bank(e):
-            return dh_banks[e % 3]
-
-        def forward(pair):
-            lo, hi = PAIR * pair, PAIR * (pair + 1)
-            xw = ring.tile([P, PAIR], U32, name="xw", align_bytes=64)
-            xs = ring.tile([P, PAIR], U8, name="xs", align_bytes=64)
-            gather(xw[:], xw_win[:].bitcast(U32), lo, hi)
-            gather(xs[:], xs_win[:], lo, hi)
-            for m in range(2):
-                e = 2 * pair + m
+        for lo, hi in cuts:
+            gather(xw, xw_win[:].bitcast(U32), lo, hi)
+        for lo, hi in cuts:
+            gather(xs, xs_win[:], lo, hi)
+            for e in range(lo // C, hi // C):
                 nc.tensor.matmul_mx(
-                    a_banks[m][:], lhsT=xw[:, slots(m)].bitcast(FP8X4), lhsT_scale=xs[:, slots(m)],
-                    rhs=w1_of(e).bitcast(FP4X4), rhs_scale=w1s[:, e, :], start=True, stop=True,
+                    banks[e % 2][:], lhsT=xw[:, slots(e)].bitcast(FP8X4), lhsT_scale=xs[:, slots(e)],
+                    rhs=w1[e // 4][:, e % 4, :].bitcast(FP4X4), rhs_scale=w1s[:, e, :], start=True, stop=True,
                 )
                 nc.scalar.activation(
                     slope[e][:].rearrange("c (u p d) -> c u p d", u=2, d=2),
-                    a_banks[m][:].rearrange("c (p u d) -> c u p d", u=2, d=2),
+                    banks[e % 2][:].rearrange("c (p u d) -> c u p d", u=2, d=2),
                     ACT.Relu, scale=2.0,
                 )
 
-        def gather_dy(pair):
-            dw = [ring.tile([P, PAIR], U32, name="dw%d" % s, align_bytes=64) for s in range(2)]
-            for s in range(2):
-                gather(dw[s][:], dw_win[:, s, :].bitcast(U32), PAIR * pair, PAIR * (pair + 1))
-            return dw
+        nc.tensor.transpose(banks[7][:, 0:P], gate_rows[:], ident[:])
+        nc.scalar.copy(gate_col[:], banks[7][:, 0:E])
 
-        def make_dh(e, dw):
-            for s, plane in enumerate((ds0, ds1)):
-                nc.tensor.matmul_mx(
-                    dh_bank(e)[:], lhsT=dw[s][:, slots(e % 2)].bitcast(FP8X4), lhsT_scale=plane[:, slots(e)],
-                    rhs=w2[e // 2][:, 2 * (e % 2) + s, :].bitcast(FP4X4), rhs_scale=w2s[:, 2 * e + s, :],
-                    start=(s == 0), stop=(s == 1),
-                )
+        def dh_bank(e):
+            return banks[(e + 2) % 8]
+
+        for lo, hi in cuts:
+            for s in range(2):
+                gather(dw[s], dw_win[:, s, :].bitcast(U32), lo, hi)
+            for e in range(lo // C, hi // C):
+                for s, plane in enumerate((ds0, ds1)):
+                    nc.tensor.matmul_mx(
+                        dh_bank(e)[:], lhsT=dw[s][:, slots(e)].bitcast(FP8X4), lhsT_scale=plane[:, slots(e)],
+                        rhs=w2[e // 2][:, 2 * (e % 2) + s, :].bitcast(FP4X4), rhs_scale=w2s[:, 2 * e + s, :],
+                        start=(s == 0), stop=(s == 1),
+                    )
 
         def make_da(e):
             for u in range(2):
@@ -169,23 +161,23 @@ def tile_moe_rec_mlp_relu2_kernel(
                     MULT, MULT,
                 )
 
-        def turn(g, bank):
-            members = groups[g]
-            for m, e in enumerate(members):
+        place = {e: (g, m) for g, members in enumerate(groups) for m, e in enumerate(members)}
+
+        def turn(experts):
+            bank = dh_bank(experts[0])
+            for j, e in enumerate(experts):
                 words = da[e][:].bitcast(F32)
                 for u in range(2):
-                    nc.tensor.transpose(bank[:, (2 * m + u) * C : (2 * m + u + 1) * C], words[:, u * P : (u + 1) * P], ident[:])
-            width = len(members) * 2 * C
+                    nc.tensor.transpose(bank[:, (2 * j + u) * C : (2 * j + u + 1) * C], words[:, u * P : (u + 1) * P], ident[:])
+            g, m = place[experts[0]]
+            width = len(experts) * 2 * C
             nc.scalar.copy(
-                da_t[g][:].bitcast(F32).rearrange("p (m c u) -> p m c u", c=C, u=2),
+                da_t[g][:].bitcast(F32)[:, m * 2 * C : m * 2 * C + width].rearrange("p (m c u) -> p m c u", c=C, u=2),
                 bank[:, 0:width].rearrange("p (m u c) -> p m c u", c=C, u=2),
             )
 
-        def quantize(g):
-            nc.vector.quantize_mx(da_codes[g][:].bitcast(FP8X4), da_scales[g][:], da_t[g][:])
-
-        def dx_product(g, m, kt, dst):
-            e = groups[g][m]
+        def dx_product(e, kt, dst):
+            g, m = place[e]
             nc.tensor.matmul_mx(
                 dst,
                 lhsT=w1t[e // 4][:, e % 4, 2 * kt * P : 2 * (kt + 1) * P].bitcast(FP4X4),
@@ -194,63 +186,30 @@ def tile_moe_rec_mlp_relu2_kernel(
                 rhs_scale=da_scales[g][:, slots(m)], start=True, stop=True,
             )
 
-        def make_dx(g):
-            for kt in range(4):
-                dst = dx_banks[kt // 2][:, (kt % 2) * PAIR : (kt % 2 + 1) * PAIR]
-                for m in range(2):
-                    dx_product(g, m, kt, dst[:, slots(m)])
-            for kt in range(4):
-                nc.scalar.copy(dx[kt][:, g * PAIR : (g + 1) * PAIR], dx_banks[kt // 2][:, (kt % 2) * PAIR : (kt % 2 + 1) * PAIR])
+        def make_dx(kt, first, last, bank, copy):
+            for e in range(first, last):
+                dx_product(e, kt, bank[:, slots(e - first)])
+            copy(dx[kt][:, first * C : last * C], bank[:, 0 : (last - first) * C])
 
-        forward(0)
-        dw = gather_dy(0)
-        make_dh(0, dw)
-        make_dh(1, dw)
-        forward(1)
-        dw = gather_dy(1)
-        make_dh(2, dw)
-        make_da(0)
-        make_dh(3, dw)
-        make_da(1)
-        turn(0, turn_bank)
-        forward(2)
-        dw = gather_dy(2)
-        make_dh(4, dw)
+        def quantize(g):
+            nc.vector.quantize_mx(da_codes[g][:].bitcast(FP8X4), da_scales[g][:], da_t[g][:])
+
+        for experts in [(0, 1), (2, 3), (4, 5)]:
+            for e in experts:
+                make_da(e)
+            turn(experts)
         quantize(0)
-        make_dx(0)
-        make_da(2)
-        make_dh(5, dw)
-        make_da(3)
-        turn(1, turn_bank)
-        forward(3)
-        dw = gather_dy(3)
-        make_dh(6, dw)
-        quantize(1)
-        make_da(4)
-        make_dh(7, dw)
-        make_dx(1)
-        make_da(5)
-        turn(2, turn_bank)
-        make_da(6)
-        turn(3, a_banks[0])
-        make_da(7)
-        turn(4, a_banks[1])
-
-        late = [(2, 0), (2, 1), (3, 0), (4, 0)]
-        late_banks = [dx_banks[0], dx_banks[1], dh_bank(6), dh_bank(7)]
-        quantize(2)
-        dx_product(2, 0, 0, late_banks[0][:, slots(0)])
-        dx_product(2, 1, 0, late_banks[0][:, slots(1)])
-        quantize(3)
-        dx_product(3, 0, 0, late_banks[0][:, slots(2)])
-        nc.scalar.copy(dx[0][:, 4 * C : 7 * C], late_banks[0][:, 0 : 3 * C])
-        quantize(4)
-        dx_product(4, 0, 0, dh_bank(5)[:, 0:C])
-        nc.scalar.copy(dx[0][:, 7 * C :], dh_bank(5)[:, 0:C])
-        for kt in range(1, 4):
-            for j, (g, m) in enumerate(late):
-                dx_product(g, m, kt, late_banks[kt][:, slots(j)])
-            nc.scalar.copy(dx[kt][:, 4 * C :], late_banks[kt][:])
+        make_dx(0, 0, 4, dh_bank(1), nc.scalar.copy)
+        for e in (6, 7):
+            make_da(e)
+            turn((e,))
+        for g in range(1, 4):
+            quantize(g)
+        make_dx(0, 4, 7, dh_bank(5), nc.scalar.copy)
+        make_dx(0, 7, 8, dh_bank(4), nc.vector.tensor_copy)
+        late_banks = [dh_bank(7), dh_bank(4), dh_bank(5)]
+        for j in range(6):
+            make_dx(1 + j // 2, 4 * (j % 2), 4 * (j % 2) + 4, late_banks[j % 3], nc.scalar.copy)
 
         first_pick = [held([P, T], F32, "first_pick%d" % kt) for kt in range(4)]
         total = [held([P, T], F32, "total%d" % kt) for kt in range(4)]

@@ -53,7 +53,7 @@ def tile_moe_rec_mlp_relu2_kernel(
         ident = held([P, P], F32, "ident")
         w1 = [held([P, 4, 2 * H], U8, "w1_%d" % h) for h in range(2)]
         w2 = [held([P, 4, 2 * H], U8, "w2_%d" % h) for h in range(4)]
-        w1t = [held([P, 4, 2 * K], U8, "w1t_%d" % h) for h in range(2)]
+        w1t = [held([P, E, K], U8, "w1t_%d" % h) for h in range(2)]
         w1s = held([P, E, H], U8, "w1s")
         w2s = held([P, 2 * E, H], U8, "w2s")
         slope = [held([P, H], F32, "slope%d" % e) for e in range(E)]
@@ -70,15 +70,15 @@ def tile_moe_rec_mlp_relu2_kernel(
         zero(nc.gpsimd, ds_win[:])
         zero(nc.gpsimd, xs_win[:])
         zero(nc.vector, w1s[:].rearrange("p e n -> p (e n)"))
-        zero(nc.vector, w2s[:].rearrange("p e n -> p (e n)"))
         nc.gpsimd.memset(gate_rows[:], 0.0)
         zero(nc.gpsimd, ds1[:])
+        zero(nc.gpsimd, w2s[:].rearrange("p e n -> p (e n)"))
         make_identity(nc, ident[:])
 
-        def load_scales(plane, rows):
+        def load_scales(plane, rows, queue):
             by_row = rows.rearrange("e s (q r) n -> r q (e s) n", r=4)
             for r in range(4):
-                nc.sync.dma_start(plane[r:P:32, :, :].bitcast(I32), by_row[r].bitcast(I32))
+                queue.dma_start(plane[r:P:32, :, :].bitcast(I32), by_row[r].bitcast(I32))
 
         def load_words(tile, words):
             nc.sync.dma_start(tile[:].bitcast(I32), words.rearrange("e s p b -> p (e s) b").bitcast(I32))
@@ -91,11 +91,11 @@ def tile_moe_rec_mlp_relu2_kernel(
         load_words(w1[1], w1_words[4:8])
         for q in range(4):
             nc.sync.dma_start(xs_win[32 * q : 32 * q + 4, :].bitcast(I32), x_scales[0, 4 * q : 4 * q + 4, :].bitcast(I32))
-        load_scales(w1s, w1_scales)
+        load_scales(w1s, w1_scales, nc.sync)
         nc.sync.dma_start(dw_win[:], dy_words.rearrange("s p t d -> p s (t d)").bitcast(I32))
         load_words(w2[0], w2t_words[0:2])
         nc.sync.dma_start(gate_rows[0:E, :], gate[0, :].rearrange("(e c) -> e c", c=C))
-        load_scales(w2s, w2t_scales)
+        load_scales(w2s, w2t_scales, nc.sync)
         for pair in range(1, 4):
             load_words(w2[pair], w2t_words[2 * pair : 2 * pair + 2])
 
@@ -109,37 +109,42 @@ def tile_moe_rec_mlp_relu2_kernel(
 
         w1ts = held([P, E, K], U8, "w1ts", tag="ds_win_then_w1ts")
         zero(nc.gpsimd, w1ts[:].rearrange("p e n -> p (e n)"))
-        load_scales(w1ts, w1t_scales)
-        load_words(w1t[0], w1t_words[0:4])
-        load_words(w1t[1], w1t_words[4:8])
+        load_scales(w1ts, w1t_scales, nc.gpsimd)
         nc.sync.dma_start(pos1_t[:], pos1)
         nc.sync.dma_start(pos2_t[:], pos2)
+        for h in range(2):
+            load_words(w1t[h], w1t_words[:, :, :, h * K : (h + 1) * K])
 
         def slots(e):
             return slice(e * C, (e + 1) * C)
 
         for lo, hi in cuts:
             gather(xw, xw_win[:].bitcast(U32), lo, hi)
+        a_banks = [banks[b] for b in (0, 1, 7, 6, 5)]
+
+        def make_slope(e):
+            nc.scalar.activation(
+                slope[e][:].rearrange("c (u p d) -> c u p d", u=2, d=2),
+                a_banks[e % 5][:].rearrange("c (p u d) -> c u p d", u=2, d=2),
+                ACT.Relu, scale=2.0,
+            )
+
         for lo, hi in cuts:
             gather(xs, xs_win[:], lo, hi)
             for e in range(lo // C, hi // C):
                 nc.tensor.matmul_mx(
-                    banks[e % 2][:], lhsT=xw[:, slots(e)].bitcast(FP8X4), lhsT_scale=xs[:, slots(e)],
+                    a_banks[e % 5][:], lhsT=xw[:, slots(e)].bitcast(FP8X4), lhsT_scale=xs[:, slots(e)],
                     rhs=w1[e // 4][:, e % 4, :].bitcast(FP4X4), rhs_scale=w1s[:, e, :], start=True, stop=True,
                 )
-                nc.scalar.activation(
-                    slope[e][:].rearrange("c (u p d) -> c u p d", u=2, d=2),
-                    banks[e % 2][:].rearrange("c (p u d) -> c u p d", u=2, d=2),
-                    ACT.Relu, scale=2.0,
-                )
+                make_slope(e)
 
-        nc.tensor.transpose(banks[7][:, 0:P], gate_rows[:], ident[:])
-        nc.scalar.copy(gate_col[:], banks[7][:, 0:E])
+        nc.tensor.transpose(banks[4][:, 0:P], gate_rows[:], ident[:])
+        nc.scalar.copy(gate_col[:], banks[4][:, 0:E])
 
         def dh_bank(e):
             return banks[(e + 2) % 8]
 
-        for lo, hi in cuts:
+        def make_dh(lo, hi):
             for s in range(2):
                 gather(dw[s], dw_win[:, s, :].bitcast(U32), lo, hi)
             for e in range(lo // C, hi // C):
@@ -180,7 +185,7 @@ def tile_moe_rec_mlp_relu2_kernel(
             g, m = place[e]
             nc.tensor.matmul_mx(
                 dst,
-                lhsT=w1t[e // 4][:, e % 4, 2 * kt * P : 2 * (kt + 1) * P].bitcast(FP4X4),
+                lhsT=w1t[kt // 2][:, e, 2 * (kt % 2) * P : 2 * (kt % 2 + 1) * P].bitcast(FP4X4),
                 lhsT_scale=w1ts[:, e, kt * P : (kt + 1) * P],
                 rhs=da_codes[g][:, slots(m)].bitcast(FP8X4),
                 rhs_scale=da_scales[g][:, slots(m)], start=True, stop=True,
@@ -194,6 +199,8 @@ def tile_moe_rec_mlp_relu2_kernel(
         def quantize(g):
             nc.vector.quantize_mx(da_codes[g][:].bitcast(FP8X4), da_scales[g][:], da_t[g][:])
 
+        for lo, hi in cuts:
+            make_dh(lo, hi)
         for experts in [(0, 1), (2, 3), (4, 5)]:
             for e in experts:
                 make_da(e)
@@ -205,8 +212,8 @@ def tile_moe_rec_mlp_relu2_kernel(
             turn((e,))
         for g in range(1, 4):
             quantize(g)
-        make_dx(0, 4, 7, dh_bank(5), nc.scalar.copy)
-        make_dx(0, 7, 8, dh_bank(4), nc.vector.tensor_copy)
+        make_dx(0, 4, 6, dh_bank(5), nc.scalar.copy)
+        make_dx(0, 6, 8, dh_bank(4), nc.vector.tensor_copy)
         late_banks = [dh_bank(7), dh_bank(4), dh_bank(5)]
         for j in range(6):
             make_dx(1 + j // 2, 4 * (j % 2), 4 * (j % 2) + 4, late_banks[j % 3], nc.scalar.copy)

@@ -31,8 +31,8 @@ def tile_moe_rec_mlp_relu2_kernel(
         keep = ctx.enter_context(tc.tile_pool(name="keep", bufs=1))
         psum = ctx.enter_context(tc.psum_pool(name="psum", bufs=1))
 
-        def held(shape, dtype, name, tag=None):
-            return keep.tile(shape, dtype, name=name, tag=tag or name, align_bytes=64)
+        def held(shape, dtype, name):
+            return keep.tile(shape, dtype, name=name, align_bytes=64)
 
         banks = [psum.tile([P, 512], F32, name="bank%d" % b) for b in range(8)]
 
@@ -42,13 +42,12 @@ def tile_moe_rec_mlp_relu2_kernel(
         xw_win = held([P, T], I32, "xw_win")
         xs_win = held([P, T], U8, "xs_win")
         dw_win = held([P, 2, T], I32, "dw_win")
-        ds_win = held([P, T], U8, "ds_win", tag="ds_win_then_w1ts")
+        ds_win = held([P, T], U8, "ds_win")
         xw = held([P, S], U32, "xw")
         xs = held([P, S], U8, "xs")
         dw = [held([P, S], U32, "dw%d" % s) for s in range(2)]
         ds0 = held([P, S], U8, "ds0")
-        ds1 = held([P, S], U8, "ds1")
-        gate_rows = held([P, C], F32, "gate_rows")
+        gate_rows = keep.tile([P, C], F32, name="gate_rows", tag="gate_then_ds1", align_bytes=64)
         gate_col = held([P, E], F32, "gate_col")
         ident = held([P, P], F32, "ident")
         w1 = [held([P, 4, 2 * H], U8, "w1_%d" % h) for h in range(2)]
@@ -69,16 +68,15 @@ def tile_moe_rec_mlp_relu2_kernel(
 
         zero(nc.gpsimd, ds_win[:])
         zero(nc.gpsimd, xs_win[:])
-        zero(nc.vector, w1s[:].rearrange("p e n -> p (e n)"))
-        nc.gpsimd.memset(gate_rows[:], 0.0)
-        zero(nc.gpsimd, ds1[:])
-        zero(nc.gpsimd, w2s[:].rearrange("p e n -> p (e n)"))
         make_identity(nc, ident[:])
+        nc.vector.memset(gate_rows[:], 0.0)
+        zero(nc.vector, w1s[:].rearrange("p e n -> p (e n)"))
+        zero(nc.vector, w2s[:].rearrange("p e n -> p (e n)"))
 
-        def load_scales(plane, rows, queue):
+        def load_scales(plane, rows):
             by_row = rows.rearrange("e s (q r) n -> r q (e s) n", r=4)
             for r in range(4):
-                queue.dma_start(plane[r:P:32, :, :].bitcast(I32), by_row[r].bitcast(I32))
+                nc.sync.dma_start(plane[r:P:32, :, :].bitcast(I32), by_row[r].bitcast(I32))
 
         def load_words(tile, words):
             nc.sync.dma_start(tile[:].bitcast(I32), words.rearrange("e s p b -> p (e s) b").bitcast(I32))
@@ -91,11 +89,11 @@ def tile_moe_rec_mlp_relu2_kernel(
         load_words(w1[1], w1_words[4:8])
         for q in range(4):
             nc.sync.dma_start(xs_win[32 * q : 32 * q + 4, :].bitcast(I32), x_scales[0, 4 * q : 4 * q + 4, :].bitcast(I32))
-        load_scales(w1s, w1_scales, nc.sync)
+        nc.sync.dma_start(gate_rows[0:E, :], gate[0, :].rearrange("(e c) -> e c", c=C))
+        load_scales(w1s, w1_scales)
         nc.sync.dma_start(dw_win[:], dy_words.rearrange("s p t d -> p s (t d)").bitcast(I32))
         load_words(w2[0], w2t_words[0:2])
-        nc.sync.dma_start(gate_rows[0:E, :], gate[0, :].rearrange("(e c) -> e c", c=C))
-        load_scales(w2s, w2t_scales, nc.sync)
+        load_scales(w2s, w2t_scales)
         for pair in range(1, 4):
             load_words(w2[pair], w2t_words[2 * pair : 2 * pair + 2])
 
@@ -105,15 +103,13 @@ def tile_moe_rec_mlp_relu2_kernel(
         cuts = [(0, 384), (384, 768), (768, 1024)]
         for lo, hi in cuts:
             gather(ds0, ds_win[:], lo, hi)
-        nc.gpsimd.dma_start(ds1[0:100, :].bitcast(I32), ds0[4:104, :].bitcast(I32))
 
-        w1ts = held([P, E, K], U8, "w1ts", tag="ds_win_then_w1ts")
-        zero(nc.gpsimd, w1ts[:].rearrange("p e n -> p (e n)"))
-        load_scales(w1ts, w1t_scales, nc.gpsimd)
-        nc.sync.dma_start(pos1_t[:], pos1)
-        nc.sync.dma_start(pos2_t[:], pos2)
-        for h in range(2):
-            load_words(w1t[h], w1t_words[:, :, :, h * K : (h + 1) * K])
+        nc.tensor.transpose(banks[4][:, 0:P], gate_rows[:], ident[:])
+        nc.scalar.copy(gate_col[:], banks[4][:, 0:E])
+
+        ds1 = keep.tile([P, S], U8, name="ds1", tag="gate_then_ds1", align_bytes=64)
+        zero(nc.gpsimd, ds1[96:P, :])
+        nc.scalar.dma_start(ds1[0:112, :].bitcast(I32), ds0[4:116, :].bitcast(I32))
 
         def slots(e):
             return slice(e * C, (e + 1) * C)
@@ -138,8 +134,13 @@ def tile_moe_rec_mlp_relu2_kernel(
                 )
                 make_slope(e)
 
-        nc.tensor.transpose(banks[4][:, 0:P], gate_rows[:], ident[:])
-        nc.scalar.copy(gate_col[:], banks[4][:, 0:E])
+        w1ts = w1s
+        nc.sync.dma_start(pos1_t[:], pos1)
+        nc.sync.dma_start(pos2_t[:], pos2)
+        load_scales(w1ts, w1t_scales)
+        for h in range(2):
+            load_words(w1t[h], w1t_words[:, :, :, h * K : (h + 1) * K])
+
 
         def dh_bank(e):
             return banks[(e + 2) % 8]

@@ -47,7 +47,8 @@ def tile_moe_rec_mlp_relu2_kernel(
         xs = held([P, S], U8, "xs")
         dw = [held([P, S], U32, "dw%d" % s) for s in range(2)]
         ds0 = held([P, S], U8, "ds0")
-        gate_rows = keep.tile([P, C], F32, name="gate_rows", tag="gate_then_ds1", align_bytes=64)
+        gate_rows = held([P, C], F32, "gate_rows")
+        ds1 = held([P, S], U8, "ds1")
         gate_col = held([P, E], F32, "gate_col")
         ident = held([P, P], F32, "ident")
         w1 = [held([P, 4, 2 * H], U8, "w1_%d" % h) for h in range(2)]
@@ -69,6 +70,7 @@ def tile_moe_rec_mlp_relu2_kernel(
         zero(nc.gpsimd, ds_win[:])
         zero(nc.gpsimd, xs_win[:])
         make_identity(nc, ident[:])
+        zero(nc.gpsimd, ds1[96:P, :])
         nc.vector.memset(gate_rows[:], 0.0)
         zero(nc.vector, w1s[:].rearrange("p e n -> p (e n)"))
         zero(nc.vector, w2s[:].rearrange("p e n -> p (e n)"))
@@ -89,13 +91,15 @@ def tile_moe_rec_mlp_relu2_kernel(
         load_words(w1[1], w1_words[4:8])
         for q in range(4):
             nc.sync.dma_start(xs_win[32 * q : 32 * q + 4, :].bitcast(I32), x_scales[0, 4 * q : 4 * q + 4, :].bitcast(I32))
-        nc.sync.dma_start(gate_rows[0:E, :], gate[0, :].rearrange("(e c) -> e c", c=C))
-        load_scales(w1s, w1_scales)
         nc.sync.dma_start(dw_win[:], dy_words.rearrange("s p t d -> p s (t d)").bitcast(I32))
+        load_scales(w1s, w1_scales)
         load_words(w2[0], w2t_words[0:2])
+        nc.sync.dma_start(gate_rows[0:E, :], gate[0, :].rearrange("(e c) -> e c", c=C))
         load_scales(w2s, w2t_scales)
-        for pair in range(1, 4):
-            load_words(w2[pair], w2t_words[2 * pair : 2 * pair + 2])
+        load_words(w2[1], w2t_words[2:4])
+        load_words(w2[2], w2t_words[4:6])
+        for m in range(2):
+            load_words(w2[3][:, 2 * m : 2 * m + 2, :], w2t_words[6 + m : 7 + m])
 
         def gather(dst, window, lo, hi):
             nc.vector.tensor_copy(dst[:, lo:hi], window.indirect(offs_t[:, lo // 16 : hi // 16]))
@@ -103,13 +107,11 @@ def tile_moe_rec_mlp_relu2_kernel(
         cuts = [(0, 384), (384, 768), (768, 1024)]
         for lo, hi in cuts:
             gather(ds0, ds_win[:], lo, hi)
+        nc.gpsimd.dma_start(ds1[0:100, :].bitcast(I32), ds0[4:104, :].bitcast(I32))
 
         nc.tensor.transpose(banks[4][:, 0:P], gate_rows[:], ident[:])
         nc.scalar.copy(gate_col[:], banks[4][:, 0:E])
 
-        ds1 = keep.tile([P, S], U8, name="ds1", tag="gate_then_ds1", align_bytes=64)
-        zero(nc.gpsimd, ds1[96:P, :])
-        nc.scalar.dma_start(ds1[0:112, :].bitcast(I32), ds0[4:116, :].bitcast(I32))
 
         def slots(e):
             return slice(e * C, (e + 1) * C)

@@ -95,11 +95,6 @@ def tile_moe_rec_mlp_relu2_kernel(
         load_scales(w1s, w1_scales)
         load_words(w2[0], w2t_words[0:2])
         nc.sync.dma_start(gate_rows[0:E, :], gate[0, :].rearrange("(e c) -> e c", c=C))
-        load_scales(w2s, w2t_scales)
-        load_words(w2[1], w2t_words[2:4])
-        load_words(w2[2], w2t_words[4:6])
-        for m in range(2):
-            load_words(w2[3][:, 2 * m : 2 * m + 2, :], w2t_words[6 + m : 7 + m])
 
         def gather(dst, window, lo, hi):
             nc.vector.tensor_copy(dst[:, lo:hi], window.indirect(offs_t[:, lo // 16 : hi // 16]))
@@ -107,7 +102,12 @@ def tile_moe_rec_mlp_relu2_kernel(
         cuts = [(0, 384), (384, 768), (768, 1024)]
         for lo, hi in cuts:
             gather(ds0, ds_win[:], lo, hi)
-        nc.gpsimd.dma_start(ds1[0:100, :].bitcast(I32), ds0[4:104, :].bitcast(I32))
+        nc.sync.dma_start(ds1[0:100, :].bitcast(I32), ds0[4:104, :].bitcast(I32))
+        load_scales(w2s, w2t_scales)
+        load_words(w2[1], w2t_words[2:4])
+        load_words(w2[2], w2t_words[4:6])
+        for m in range(2):
+            load_words(w2[3][:, 2 * m : 2 * m + 2, :], w2t_words[6 + m : 7 + m])
 
         nc.tensor.transpose(banks[4][:, 0:P], gate_rows[:], ident[:])
         nc.scalar.copy(gate_col[:], banks[4][:, 0:E])

@@ -70,15 +70,15 @@ def tile_moe_rec_mlp_relu2_kernel(
         zero(nc.gpsimd, ds_win[:])
         zero(nc.gpsimd, xs_win[:])
         make_identity(nc, ident[:])
-        zero(nc.gpsimd, ds1[96:P, :])
+        zero(nc.gpsimd, ds1[:])
         nc.vector.memset(gate_rows[:], 0.0)
         zero(nc.vector, w1s[:].rearrange("p e n -> p (e n)"))
         zero(nc.vector, w2s[:].rearrange("p e n -> p (e n)"))
 
-        def load_scales(plane, rows):
+        def load_scales(plane, rows, cols=slice(0, H)):
             by_row = rows.rearrange("e s (q r) n -> r q (e s) n", r=4)
             for r in range(4):
-                nc.sync.dma_start(plane[r:P:32, :, :].bitcast(I32), by_row[r].bitcast(I32))
+                nc.sync.dma_start(plane[r:P:32, :, cols].bitcast(I32), by_row[r][:, :, cols].bitcast(I32))
 
         def load_words(tile, words):
             nc.sync.dma_start(tile[:].bitcast(I32), words.rearrange("e s p b -> p (e s) b").bitcast(I32))
@@ -92,9 +92,9 @@ def tile_moe_rec_mlp_relu2_kernel(
         for q in range(4):
             nc.sync.dma_start(xs_win[32 * q : 32 * q + 4, :].bitcast(I32), x_scales[0, 4 * q : 4 * q + 4, :].bitcast(I32))
         nc.sync.dma_start(dw_win[:], dy_words.rearrange("s p t d -> p s (t d)").bitcast(I32))
-        load_scales(w1s, w1_scales)
-        load_words(w2[0], w2t_words[0:2])
         nc.sync.dma_start(gate_rows[0:E, :], gate[0, :].rearrange("(e c) -> e c", c=C))
+        load_scales(w1s, w1_scales)
+        load_scales(w2s, w2t_scales)
 
         def gather(dst, window, lo, hi):
             nc.vector.tensor_copy(dst[:, lo:hi], window.indirect(offs_t[:, lo // 16 : hi // 16]))
@@ -102,8 +102,9 @@ def tile_moe_rec_mlp_relu2_kernel(
         cuts = [(0, 384), (384, 768), (768, 1024)]
         for lo, hi in cuts:
             gather(ds0, ds_win[:], lo, hi)
-        nc.sync.dma_start(ds1[0:100, :].bitcast(I32), ds0[4:104, :].bitcast(I32))
-        load_scales(w2s, w2t_scales)
+        for r in range(4):
+            nc.sync.dma_start(ds1[r:P:32, :].bitcast(I32), ds0[4 + r : P : 32, :].bitcast(I32))
+        load_words(w2[0], w2t_words[0:2])
         load_words(w2[1], w2t_words[2:4])
         load_words(w2[2], w2t_words[4:6])
         for m in range(2):
@@ -139,8 +140,8 @@ def tile_moe_rec_mlp_relu2_kernel(
         w1ts = w1s
         nc.sync.dma_start(pos1_t[:], pos1)
         nc.sync.dma_start(pos2_t[:], pos2)
-        load_scales(w1ts, w1t_scales)
         for h in range(2):
+            load_scales(w1ts, w1t_scales, slice(h * 2 * P, (h + 1) * 2 * P))
             load_words(w1t[h], w1t_words[:, :, :, h * K : (h + 1) * K])
 
 

@@ -53,7 +53,9 @@ def tile_moe_rec_mlp_relu2_kernel(
         ident = held([P, P], F32, "ident")
         w1 = [held([P, 4, 2 * H], U8, "w1_%d" % h) for h in range(2)]
         w2 = [held([P, 4, 2 * H], U8, "w2_%d" % h) for h in range(4)]
-        w1t = [held([P, E, K], U8, "w1t_%d" % h) for h in range(2)]
+        w1t_first = [held([P, E // 2, 2 * P], U8, "w1t_first%d" % h) for h in range(2)]
+        w1t_second = held([P, E, 2 * P], U8, "w1t_second")
+        w1t_rest = held([P, E, 4 * P], U8, "w1t_rest")
         w1s = held([P, E, H], U8, "w1s")
         w2s = held([P, 2 * E, H], U8, "w2s")
         slope = [held([P, H], F32, "slope%d" % e) for e in range(E)]
@@ -84,9 +86,9 @@ def tile_moe_rec_mlp_relu2_kernel(
             nc.sync.dma_start(tile[:].bitcast(I32), words.rearrange("e s p b -> p (e s) b").bitcast(I32))
 
         nc.sync.dma_start(offs_t[:], offs)
+        nc.sync.dma_start(xw_win[:], x_words[0].rearrange("p t d -> p (t d)").bitcast(I32))
         for q in range(4):
             nc.sync.dma_start(ds_win[32 * q : 32 * q + 8, :].bitcast(I32), dy_scales[:, 4 * q : 4 * q + 4, :].bitcast(I32))
-        nc.sync.dma_start(xw_win[:], x_words[0].rearrange("p t d -> p (t d)").bitcast(I32))
         load_words(w1[0], w1_words[0:4])
         load_words(w1[1], w1_words[4:8])
         for q in range(4):
@@ -100,6 +102,8 @@ def tile_moe_rec_mlp_relu2_kernel(
             nc.vector.tensor_copy(dst[:, lo:hi], window.indirect(offs_t[:, lo // 16 : hi // 16]))
 
         cuts = [(0, 384), (384, 768), (768, 1024)]
+        for lo, hi in cuts:
+            gather(xw, xw_win[:].bitcast(U32), lo, hi)
         for lo, hi in cuts:
             gather(ds0, ds_win[:], lo, hi)
         for r in range(4):
@@ -117,8 +121,6 @@ def tile_moe_rec_mlp_relu2_kernel(
         def slots(e):
             return slice(e * C, (e + 1) * C)
 
-        for lo, hi in cuts:
-            gather(xw, xw_win[:].bitcast(U32), lo, hi)
         a_banks = [banks[b] for b in (0, 1, 7, 6, 5)]
 
         def make_slope(e):
@@ -140,18 +142,25 @@ def tile_moe_rec_mlp_relu2_kernel(
         w1ts = w1s
         nc.sync.dma_start(pos1_t[:], pos1)
         nc.sync.dma_start(pos2_t[:], pos2)
+        load_scales(w1ts, w1t_scales, slice(0, 2 * P))
         for h in range(2):
-            load_scales(w1ts, w1t_scales, slice(h * 2 * P, (h + 1) * 2 * P))
-            load_words(w1t[h], w1t_words[:, :, :, h * K : (h + 1) * K])
+            load_words(w1t_first[h], w1t_words[4 * h : 4 * h + 4, :, :, 0 : 2 * P])
+        load_words(w1t_second, w1t_words[:, :, :, 2 * P : 4 * P])
+        load_scales(w1ts, w1t_scales, slice(2 * P, 4 * P))
+        load_words(w1t_rest, w1t_words[:, :, :, 4 * P : 8 * P])
 
+        def w1t_columns(e, kt):
+            if kt == 0:
+                return w1t_first[e // 4][:, e % 4, :]
+            if kt == 1:
+                return w1t_second[:, e, :]
+            return w1t_rest[:, e, 2 * P * (kt - 2) : 2 * P * (kt - 1)]
 
         def dh_bank(e):
             return banks[(e + 2) % 8]
 
-        def make_dh(lo, hi):
-            for s in range(2):
-                gather(dw[s], dw_win[:, s, :].bitcast(U32), lo, hi)
-            for e in range(lo // C, hi // C):
+        def make_dh(experts):
+            for e in experts:
                 for s, plane in enumerate((ds0, ds1)):
                     nc.tensor.matmul_mx(
                         dh_bank(e)[:], lhsT=dw[s][:, slots(e)].bitcast(FP8X4), lhsT_scale=plane[:, slots(e)],
@@ -189,7 +198,7 @@ def tile_moe_rec_mlp_relu2_kernel(
             g, m = place[e]
             nc.tensor.matmul_mx(
                 dst,
-                lhsT=w1t[kt // 2][:, e, 2 * (kt % 2) * P : 2 * (kt % 2 + 1) * P].bitcast(FP4X4),
+                lhsT=w1t_columns(e, kt).bitcast(FP4X4),
                 lhsT_scale=w1ts[:, e, kt * P : (kt + 1) * P],
                 rhs=da_codes[g][:, slots(m)].bitcast(FP8X4),
                 rhs_scale=da_scales[g][:, slots(m)], start=True, stop=True,
@@ -204,18 +213,21 @@ def tile_moe_rec_mlp_relu2_kernel(
             nc.vector.quantize_mx(da_codes[g][:].bitcast(FP8X4), da_scales[g][:], da_t[g][:])
 
         for lo, hi in cuts:
-            make_dh(lo, hi)
-        for experts in [(0, 1), (2, 3), (4, 5)]:
-            for e in experts:
-                make_da(e)
-            turn(experts)
-        quantize(0)
-        make_dx(0, 0, 4, dh_bank(1), nc.scalar.copy)
+            for s in range(2):
+                gather(dw[s], dw_win[:, s, :].bitcast(U32), lo, hi)
+        make_dh((0, 1, 2, 3))
+        for first in (0, 2, 4):
+            make_da(first)
+            make_da(first + 1)
+            turn((first, first + 1))
+            if first < 4:
+                make_dh((first + 4, first + 5))
         for e in (6, 7):
             make_da(e)
             turn((e,))
-        for g in range(1, 4):
+        for g in range(4):
             quantize(g)
+        make_dx(0, 0, 4, dh_bank(1), nc.scalar.copy)
         make_dx(0, 4, 6, dh_bank(5), nc.scalar.copy)
         make_dx(0, 6, 8, dh_bank(4), nc.vector.tensor_copy)
         late_banks = [dh_bank(7), dh_bank(4), dh_bank(5)]
@@ -225,8 +237,8 @@ def tile_moe_rec_mlp_relu2_kernel(
         first_pick = [held([P, T], F32, "first_pick%d" % kt) for kt in range(4)]
         total = [held([P, T], F32, "total%d" % kt) for kt in range(4)]
 
-        def pick(kt):
-            nc.vector.tensor_copy(first_pick[kt][:], dx[kt][:].indirect(pos1_t[:]))
+        def pick(kt, lo, hi):
+            nc.vector.tensor_copy(first_pick[kt][:, lo:hi], dx[kt][:].indirect(pos1_t[:, lo // 16 : hi // 16]))
 
         def finish(kt, lo, hi):
             nc.vector.tensor_tensor(
@@ -234,9 +246,14 @@ def tile_moe_rec_mlp_relu2_kernel(
             )
             nc.sync.dma_start(out[kt * P : (kt + 1) * P, lo:hi], total[kt][:, lo:hi])
 
-        pick(0)
-        for kt in range(3):
-            pick(kt + 1)
-            finish(kt, 0, T)
-        finish(3, 0, T // 2)
-        finish(3, T // 2, T)
+        halves = [(0, T // 2), (T // 2, T)]
+        for kt in range(2):
+            for lo, hi in halves:
+                pick(kt, lo, hi)
+            for lo, hi in halves:
+                finish(kt, lo, hi)
+        pick(2, 0, T)
+        pick(3, 0, T)
+        finish(2, 0, T)
+        for lo, hi in halves:
+            finish(3, lo, hi)

@@ -54,8 +54,7 @@ def tile_moe_rec_mlp_relu2_kernel(
         w1 = [held([P, 4, 2 * H], U8, "w1_%d" % h) for h in range(2)]
         w2 = [held([P, 4, 2 * H], U8, "w2_%d" % h) for h in range(4)]
         w1t_first = [held([P, E // 2, 2 * P], U8, "w1t_first%d" % h) for h in range(2)]
-        w1t_second = held([P, E, 2 * P], U8, "w1t_second")
-        w1t_rest = held([P, E, 4 * P], U8, "w1t_rest")
+        w1t_later = [held([P, E, 2 * P], U8, "w1t_later%d" % kt) for kt in range(1, 4)]
         w1s = held([P, E, H], U8, "w1s")
         w2s = held([P, 2 * E, H], U8, "w2s")
         slope = [held([P, H], F32, "slope%d" % e) for e in range(E)]
@@ -80,7 +79,7 @@ def tile_moe_rec_mlp_relu2_kernel(
         def load_scales(plane, rows, cols=slice(0, H)):
             by_row = rows.rearrange("e s (q r) n -> r q (e s) n", r=4)
             for r in range(4):
-                nc.sync.dma_start(plane[r:P:32, :, cols].bitcast(I32), by_row[r][:, :, cols].bitcast(I32))
+                nc.sync.dma_start(plane[r:P:32, :, :].bitcast(I32), by_row[r][:, :, cols].bitcast(I32))
 
         def load_words(tile, words):
             nc.sync.dma_start(tile[:].bitcast(I32), words.rearrange("e s p b -> p (e s) b").bitcast(I32))
@@ -139,22 +138,21 @@ def tile_moe_rec_mlp_relu2_kernel(
                 )
                 make_slope(e)
 
-        w1ts = w1s
-        nc.sync.dma_start(pos1_t[:], pos1)
-        nc.sync.dma_start(pos2_t[:], pos2)
-        load_scales(w1ts, w1t_scales, slice(0, 2 * P))
+        w1ts = [w1s[:, 4 * h : 4 * h + 4, :].rearrange("p e (j n) -> p (e j) n", j=2) for h in range(2)]
+        load_scales(w1ts[0], w1t_scales, slice(0, 2 * P))
         for h in range(2):
             load_words(w1t_first[h], w1t_words[4 * h : 4 * h + 4, :, :, 0 : 2 * P])
-        load_words(w1t_second, w1t_words[:, :, :, 2 * P : 4 * P])
-        load_scales(w1ts, w1t_scales, slice(2 * P, 4 * P))
-        load_words(w1t_rest, w1t_words[:, :, :, 4 * P : 8 * P])
+        nc.sync.dma_start(pos1_t[:], pos1)
+        nc.sync.dma_start(pos2_t[:], pos2)
+        for kt in range(1, 4):
+            if kt == 2:
+                load_scales(w1ts[1], w1t_scales, slice(2 * P, 4 * P))
+            load_words(w1t_later[kt - 1], w1t_words[:, :, :, 2 * P * kt : 2 * P * (kt + 1)])
 
         def w1t_columns(e, kt):
             if kt == 0:
                 return w1t_first[e // 4][:, e % 4, :]
-            if kt == 1:
-                return w1t_second[:, e, :]
-            return w1t_rest[:, e, 2 * P * (kt - 2) : 2 * P * (kt - 1)]
+            return w1t_later[kt - 1][:, e, :]
 
         def dh_bank(e):
             return banks[(e + 2) % 8]
@@ -199,7 +197,7 @@ def tile_moe_rec_mlp_relu2_kernel(
             nc.tensor.matmul_mx(
                 dst,
                 lhsT=w1t_columns(e, kt).bitcast(FP4X4),
-                lhsT_scale=w1ts[:, e, kt * P : (kt + 1) * P],
+                lhsT_scale=w1ts[kt // 2][:, e, (kt % 2) * P : (kt % 2 + 1) * P],
                 rhs=da_codes[g][:, slots(m)].bitcast(FP8X4),
                 rhs_scale=da_scales[g][:, slots(m)], start=True, stop=True,
             )
@@ -222,14 +220,15 @@ def tile_moe_rec_mlp_relu2_kernel(
             turn((first, first + 1))
             if first < 4:
                 make_dh((first + 4, first + 5))
+        quantize(0)
         for e in (6, 7):
             make_da(e)
             turn((e,))
-        for g in range(4):
+        for g in range(1, 4):
             quantize(g)
         make_dx(0, 0, 4, dh_bank(1), nc.scalar.copy)
-        make_dx(0, 4, 6, dh_bank(5), nc.scalar.copy)
-        make_dx(0, 6, 8, dh_bank(4), nc.vector.tensor_copy)
+        make_dx(0, 4, 7, dh_bank(5), nc.scalar.copy)
+        make_dx(0, 7, 8, dh_bank(4), nc.vector.tensor_copy)
         late_banks = [dh_bank(7), dh_bank(4), dh_bank(5)]
         for j in range(6):
             make_dx(1 + j // 2, 4 * (j % 2), 4 * (j % 2) + 4, late_banks[j % 3], nc.scalar.copy)

@@ -6,7 +6,7 @@ from concourse.masks import make_identity
 K, T, E, C, H, N = 512, 512, 8, 128, 512, 1024
 S = E * C
 P = 128
-PAIR = 2 * C
+ROW_TILES = K // P
 FLOPS = 2 * S * (K * H + N * H + H * K)
 
 F32 = mybir.dt.float32
@@ -46,24 +46,25 @@ def tile_moe_rec_mlp_relu2_kernel(
         xw = held([P, S], U32, "xw")
         xs = held([P, S], U8, "xs")
         dw = [held([P, S], U32, "dw%d" % s) for s in range(2)]
-        ds0 = held([P, S], U8, "ds0")
+        ds = [held([P, S], U8, "ds%d" % s) for s in range(2)]
         gate_rows = held([P, C], F32, "gate_rows")
-        ds1 = held([P, S], U8, "ds1")
         gate_col = held([P, E], F32, "gate_col")
         ident = held([P, P], F32, "ident")
         w1 = [held([P, 4, 2 * H], U8, "w1_%d" % h) for h in range(2)]
         w2 = [held([P, 4, 2 * H], U8, "w2_%d" % h) for h in range(4)]
-        w1t_first = [held([P, E // 2, 2 * P], U8, "w1t_first%d" % h) for h in range(2)]
-        w1t_later = [held([P, E, 2 * P], U8, "w1t_later%d" % kt) for kt in range(1, 4)]
+        groups = [(0, 1, 2, 3), (4, 5), (6, 7)]
+        w1t = [held([P, len(g), 2 * K], U8, "w1t_%d" % g[0]) for g in groups]
         w1s = held([P, E, H], U8, "w1s")
         w2s = held([P, 2 * E, H], U8, "w2s")
         slope = [held([P, H], F32, "slope%d" % e) for e in range(E)]
         da = [held([P, H], BF16, "da%d" % e) for e in range(E)]
-        groups = [(0, 1, 2, 3), (4, 5), (6,), (7,)]
-        da_t = [held([P, len(g) * C * 4], BF16, "da_t%d" % g[0]) for g in groups]
-        da_codes = [held([P, len(g) * C], U32, "da_codes%d" % g[0]) for g in groups]
-        da_scales = [held([P, len(g) * C], U8, "da_scales%d" % g[0]) for g in groups]
-        dx = [held([P, S], F32, "dx%d" % kt) for kt in range(4)]
+        lots = [(0, 1, 2, 3), (4, 5), (6,), (7,)]
+        da_t = [held([P, len(g) * C * 4], BF16, "da_t%d" % g[0]) for g in lots]
+        da_codes = [held([P, len(g) * C], U32, "da_codes%d" % g[0]) for g in lots]
+        da_scales = [held([P, len(g) * C], U8, "da_scales%d" % g[0]) for g in lots]
+        dx = [held([P, S], F32, "dx%d" % kt) for kt in range(ROW_TILES)]
+        first_pick = [held([P, T], F32, "first_pick%d" % kt) for kt in range(ROW_TILES)]
+        total = [held([P, T], F32, "total%d" % kt) for kt in range(ROW_TILES)]
 
         def zero(engine, plane):
             engine.memset(plane.bitcast(I32), 0)
@@ -71,25 +72,25 @@ def tile_moe_rec_mlp_relu2_kernel(
         zero(nc.gpsimd, ds_win[:])
         zero(nc.gpsimd, xs_win[:])
         make_identity(nc, ident[:])
-        zero(nc.gpsimd, ds1[:])
+        zero(nc.gpsimd, ds[1][:])
         nc.vector.memset(gate_rows[:], 0.0)
         zero(nc.vector, w1s[:].rearrange("p e n -> p (e n)"))
         zero(nc.vector, w2s[:].rearrange("p e n -> p (e n)"))
 
-        def load_scales(plane, rows, cols=slice(0, H)):
+        def load_scales(plane, rows):
             by_row = rows.rearrange("e s (q r) n -> r q (e s) n", r=4)
             for r in range(4):
-                nc.sync.dma_start(plane[r:P:32, :, :].bitcast(I32), by_row[r][:, :, cols].bitcast(I32))
+                nc.sync.dma_start(plane[r:P:32, :, :].bitcast(I32), by_row[r].bitcast(I32))
 
         def load_words(tile, words):
-            nc.sync.dma_start(tile[:].bitcast(I32), words.rearrange("e s p b -> p (e s) b").bitcast(I32))
+            nc.sync.dma_start(tile.bitcast(I32), words.rearrange("e s p b -> p (e s) b").bitcast(I32))
 
         nc.sync.dma_start(offs_t[:], offs)
         nc.sync.dma_start(xw_win[:], x_words[0].rearrange("p t d -> p (t d)").bitcast(I32))
         for q in range(4):
             nc.sync.dma_start(ds_win[32 * q : 32 * q + 8, :].bitcast(I32), dy_scales[:, 4 * q : 4 * q + 4, :].bitcast(I32))
-        load_words(w1[0], w1_words[0:4])
-        load_words(w1[1], w1_words[4:8])
+        load_words(w1[0][:], w1_words[0:4])
+        load_words(w1[1][:], w1_words[4:8])
         for q in range(4):
             nc.sync.dma_start(xs_win[32 * q : 32 * q + 4, :].bitcast(I32), x_scales[0, 4 * q : 4 * q + 4, :].bitcast(I32))
         nc.sync.dma_start(dw_win[:], dy_words.rearrange("s p t d -> p s (t d)").bitcast(I32))
@@ -104,155 +105,127 @@ def tile_moe_rec_mlp_relu2_kernel(
         for lo, hi in cuts:
             gather(xw, xw_win[:].bitcast(U32), lo, hi)
         for lo, hi in cuts:
-            gather(ds0, ds_win[:], lo, hi)
+            gather(ds[0], ds_win[:], lo, hi)
         for r in range(4):
-            nc.sync.dma_start(ds1[r:P:32, :].bitcast(I32), ds0[4 + r : P : 32, :].bitcast(I32))
-        load_words(w2[0], w2t_words[0:2])
-        load_words(w2[1], w2t_words[2:4])
-        load_words(w2[2], w2t_words[4:6])
-        for m in range(2):
-            load_words(w2[3][:, 2 * m : 2 * m + 2, :], w2t_words[6 + m : 7 + m])
+            nc.sync.dma_start(ds[1][r:P:32, :].bitcast(I32), ds[0][4 + r : P : 32, :].bitcast(I32))
+        for h in range(4):
+            load_words(w2[h][:], w2t_words[2 * h : 2 * h + 2])
 
-        nc.tensor.transpose(banks[4][:, 0:P], gate_rows[:], ident[:])
-        nc.scalar.copy(gate_col[:], banks[4][:, 0:E])
-
+        nc.tensor.transpose(banks[7][:, 0:P], gate_rows[:], ident[:])
+        nc.scalar.copy(gate_col[:], banks[7][:, 0:E])
 
         def slots(e):
             return slice(e * C, (e + 1) * C)
-
-        a_banks = [banks[b] for b in (0, 1, 7, 6, 5)]
-
-        def make_slope(e):
-            nc.scalar.activation(
-                slope[e][:].rearrange("c (u p d) -> c u p d", u=2, d=2),
-                a_banks[e % 5][:].rearrange("c (p u d) -> c u p d", u=2, d=2),
-                ACT.Relu, scale=2.0,
-            )
 
         for lo, hi in cuts:
             gather(xs, xs_win[:], lo, hi)
             for e in range(lo // C, hi // C):
                 nc.tensor.matmul_mx(
-                    a_banks[e % 5][:], lhsT=xw[:, slots(e)].bitcast(FP8X4), lhsT_scale=xs[:, slots(e)],
+                    banks[e][:], lhsT=xw[:, slots(e)].bitcast(FP8X4), lhsT_scale=xs[:, slots(e)],
                     rhs=w1[e // 4][:, e % 4, :].bitcast(FP4X4), rhs_scale=w1s[:, e, :], start=True, stop=True,
                 )
-                make_slope(e)
+                nc.scalar.activation(
+                    slope[e][:].rearrange("c (u p d) -> c u p d", u=2, d=2),
+                    banks[e][:].rearrange("c (p u d) -> c u p d", u=2, d=2),
+                    ACT.Relu, scale=2.0,
+                )
 
-        w1ts = [w1s[:, 4 * h : 4 * h + 4, :].rearrange("p e (j n) -> p (e j) n", j=2) for h in range(2)]
-        load_scales(w1ts[0], w1t_scales, slice(0, 2 * P))
-        for h in range(2):
-            load_words(w1t_first[h], w1t_words[4 * h : 4 * h + 4, :, :, 0 : 2 * P])
-        nc.sync.dma_start(pos1_t[:], pos1)
-        nc.sync.dma_start(pos2_t[:], pos2)
-        for kt in range(1, 4):
-            if kt == 2:
-                load_scales(w1ts[1], w1t_scales, slice(2 * P, 4 * P))
-            load_words(w1t_later[kt - 1], w1t_words[:, :, :, 2 * P * kt : 2 * P * (kt + 1)])
+        w1ts = w1s
+        load_scales(w1ts, w1t_scales)
+        for g, members in enumerate(groups):
+            load_words(w1t[g][:], w1t_words[members[0] : members[-1] + 1])
+            if g == 0:
+                nc.sync.dma_start(pos1_t[:], pos1)
+                nc.sync.dma_start(pos2_t[:], pos2)
 
-        def w1t_columns(e, kt):
-            if kt == 0:
-                return w1t_first[e // 4][:, e % 4, :]
-            return w1t_later[kt - 1][:, e, :]
-
-        def dh_bank(e):
-            return banks[(e + 2) % 8]
-
-        def make_dh(experts):
-            for e in experts:
-                for s, plane in enumerate((ds0, ds1)):
-                    nc.tensor.matmul_mx(
-                        dh_bank(e)[:], lhsT=dw[s][:, slots(e)].bitcast(FP8X4), lhsT_scale=plane[:, slots(e)],
-                        rhs=w2[e // 2][:, 2 * (e % 2) + s, :].bitcast(FP4X4), rhs_scale=w2s[:, 2 * e + s, :],
-                        start=(s == 0), stop=(s == 1),
-                    )
+        def make_dh(e):
+            for s in range(2):
+                nc.tensor.matmul_mx(
+                    banks[e][:], lhsT=dw[s][:, slots(e)].bitcast(FP8X4), lhsT_scale=ds[s][:, slots(e)],
+                    rhs=w2[e // 2][:, 2 * (e % 2) + s, :].bitcast(FP4X4), rhs_scale=w2s[:, 2 * e + s, :],
+                    start=(s == 0), stop=(s == 1),
+                )
 
         def make_da(e):
             for u in range(2):
                 half = slice(u * 2 * P, (u + 1) * 2 * P)
                 nc.vector.scalar_tensor_tensor(
                     da[e][:, half].rearrange("c (p d) -> c p d", d=2),
-                    dh_bank(e)[:].rearrange("c (p u d) -> c u p d", u=2, d=2)[:, u],
+                    banks[e][:].rearrange("c (p u d) -> c u p d", u=2, d=2)[:, u],
                     gate_col[:, e : e + 1],
                     slope[e][:, half].rearrange("c (p d) -> c p d", d=2),
                     MULT, MULT,
                 )
 
-        place = {e: (g, m) for g, members in enumerate(groups) for m, e in enumerate(members)}
+        lot_of = {e: (g, m) for g, members in enumerate(lots) for m, e in enumerate(members)}
+        group_of = {e: (g, m) for g, members in enumerate(groups) for m, e in enumerate(members)}
 
         def turn(experts):
-            bank = dh_bank(experts[0])
+            bank = banks[experts[0]]
             for j, e in enumerate(experts):
                 words = da[e][:].bitcast(F32)
                 for u in range(2):
                     nc.tensor.transpose(bank[:, (2 * j + u) * C : (2 * j + u + 1) * C], words[:, u * P : (u + 1) * P], ident[:])
-            g, m = place[experts[0]]
+            g, m = lot_of[experts[0]]
             width = len(experts) * 2 * C
             nc.scalar.copy(
                 da_t[g][:].bitcast(F32)[:, m * 2 * C : m * 2 * C + width].rearrange("p (m c u) -> p m c u", c=C, u=2),
                 bank[:, 0:width].rearrange("p (m u c) -> p m c u", c=C, u=2),
             )
 
+        def quantize(g):
+            nc.vector.quantize_mx(da_codes[g][:].bitcast(FP8X4), da_scales[g][:], da_t[g][:])
+
         def dx_product(e, kt, dst):
-            g, m = place[e]
+            g, m = lot_of[e]
+            wg, wm = group_of[e]
             nc.tensor.matmul_mx(
                 dst,
-                lhsT=w1t_columns(e, kt).bitcast(FP4X4),
-                lhsT_scale=w1ts[kt // 2][:, e, (kt % 2) * P : (kt % 2 + 1) * P],
+                lhsT=w1t[wg][:, wm, 2 * P * kt : 2 * P * (kt + 1)].bitcast(FP4X4),
+                lhsT_scale=w1ts[:, e, kt * P : (kt + 1) * P],
                 rhs=da_codes[g][:, slots(m)].bitcast(FP8X4),
                 rhs_scale=da_scales[g][:, slots(m)], start=True, stop=True,
             )
 
-        def make_dx(kt, first, last, bank, copy):
-            for e in range(first, last):
-                dx_product(e, kt, bank[:, slots(e - first)])
-            copy(dx[kt][:, first * C : last * C], bank[:, 0 : (last - first) * C])
+        def make_dx(experts, row_tiles, bank, copies):
+            width = len(experts) * C
+            for e in experts:
+                for j, kt in enumerate(row_tiles):
+                    at = j * width + (e - experts[0]) * C
+                    dx_product(e, kt, bank[:, at : at + C])
+            for j, kt in enumerate(row_tiles):
+                copies[j](dx[kt][:, experts[0] * C : experts[0] * C + width], bank[:, j * width : (j + 1) * width])
 
-        def quantize(g):
-            nc.vector.quantize_mx(da_codes[g][:].bitcast(FP8X4), da_scales[g][:], da_t[g][:])
+        on_scalar, on_vector = nc.scalar.copy, nc.vector.tensor_copy
 
         for lo, hi in cuts:
             for s in range(2):
                 gather(dw[s], dw_win[:, s, :].bitcast(U32), lo, hi)
-        make_dh((0, 1, 2, 3))
+        for e in range(E):
+            make_dh(e)
         for first in (0, 2, 4):
             make_da(first)
             make_da(first + 1)
             turn((first, first + 1))
-            if first < 4:
-                make_dh((first + 4, first + 5))
         quantize(0)
-        for e in (6, 7):
-            make_da(e)
-            turn((e,))
+        make_da(6)
+        turn((6,))
+        make_da(7)
+        turn((7,))
+        for kt, b in enumerate((1, 3, 0, 2)):
+            make_dx(groups[0], (kt,), banks[b], (on_scalar,))
         for g in range(1, 4):
             quantize(g)
-        make_dx(0, 0, 4, dh_bank(1), nc.scalar.copy)
-        make_dx(0, 4, 7, dh_bank(5), nc.scalar.copy)
-        make_dx(0, 7, 8, dh_bank(4), nc.vector.tensor_copy)
-        late_banks = [dh_bank(7), dh_bank(4), dh_bank(5)]
-        for j in range(6):
-            make_dx(1 + j // 2, 4 * (j % 2), 4 * (j % 2) + 4, late_banks[j % 3], nc.scalar.copy)
-
-        first_pick = [held([P, T], F32, "first_pick%d" % kt) for kt in range(4)]
-        total = [held([P, T], F32, "total%d" % kt) for kt in range(4)]
-
-        def pick(kt, lo, hi):
-            nc.vector.tensor_copy(first_pick[kt][:, lo:hi], dx[kt][:].indirect(pos1_t[:, lo // 16 : hi // 16]))
-
-        def finish(kt, lo, hi):
-            nc.vector.tensor_tensor(
-                total[kt][:, lo:hi], dx[kt][:].indirect(pos2_t[:, lo // 16 : hi // 16]), first_pick[kt][:, lo:hi], ADD
-            )
-            nc.sync.dma_start(out[kt * P : (kt + 1) * P, lo:hi], total[kt][:, lo:hi])
+        make_dx(groups[1], (0, 1), banks[5], (on_vector, on_vector))
+        make_dx(groups[1], (2, 3), banks[4], (on_vector, on_vector))
+        make_dx(groups[2], (0, 1), banks[6], (on_scalar, on_vector))
+        make_dx(groups[2], (2, 3), banks[7], (on_vector, on_vector))
 
         halves = [(0, T // 2), (T // 2, T)]
-        for kt in range(2):
+        for kt in range(ROW_TILES):
             for lo, hi in halves:
-                pick(kt, lo, hi)
-            for lo, hi in halves:
-                finish(kt, lo, hi)
-        pick(2, 0, T)
-        pick(3, 0, T)
-        finish(2, 0, T)
-        for lo, hi in halves:
-            finish(3, lo, hi)
+                nc.scalar.activation(first_pick[kt][:, lo:hi], dx[kt][:].indirect(pos1_t[:, lo // 16 : hi // 16]), ACT.Copy)
+                nc.vector.tensor_tensor(
+                    total[kt][:, lo:hi], dx[kt][:].indirect(pos2_t[:, lo // 16 : hi // 16]), first_pick[kt][:, lo:hi], ADD
+                )
+                nc.sync.dma_start(out[kt * P : (kt + 1) * P, lo:hi], total[kt][:, lo:hi])

@@ -52,13 +52,13 @@ def tile_moe_rec_mlp_relu2_kernel(
         ident = held([P, P], F32, "ident")
         w1 = [held([P, 4, 2 * H], U8, "w1_%d" % h) for h in range(2)]
         w2 = [held([P, 4, 2 * H], U8, "w2_%d" % h) for h in range(4)]
-        groups = [(0, 1, 2, 3), (4, 5), (6, 7)]
-        w1t = [held([P, len(g), 2 * K], U8, "w1t_%d" % g[0]) for g in groups]
+        w1t = [held([P, 4, 2 * K], U8, "w1t_%d" % h) for h in range(2)]
         w1s = held([P, E, H], U8, "w1s")
         w2s = held([P, 2 * E, H], U8, "w2s")
         slope = [held([P, H], F32, "slope%d" % e) for e in range(E)]
         da = [held([P, H], BF16, "da%d" % e) for e in range(E)]
-        lots = [(0, 1, 2, 3), (4, 5), (6,), (7,)]
+        dh_gated = {e: held([P, H], F32, "dh_gated%d" % e) for e in (6, 7)}
+        lots = [(0, 1, 2, 3), (4, 5, 6, 7)]
         da_t = [held([P, len(g) * C * 4], BF16, "da_t%d" % g[0]) for g in lots]
         da_codes = [held([P, len(g) * C], U32, "da_codes%d" % g[0]) for g in lots]
         da_scales = [held([P, len(g) * C], U8, "da_scales%d" % g[0]) for g in lots]
@@ -75,7 +75,11 @@ def tile_moe_rec_mlp_relu2_kernel(
         zero(nc.gpsimd, ds[1][:])
         nc.vector.memset(gate_rows[:], 0.0)
         zero(nc.vector, w1s[:].rearrange("p e n -> p (e n)"))
-        zero(nc.vector, w2s[:].rearrange("p e n -> p (e n)"))
+        for h in range(2):
+            nc.scalar.copy(
+                w2s[:, h * E : (h + 1) * E, :].rearrange("p e n -> p (e n)").bitcast(U32),
+                w1s[:].rearrange("p e n -> p (e n)").bitcast(U32),
+            )
 
         def load_scales(plane, rows):
             by_row = rows.rearrange("e s (q r) n -> r q (e s) n", r=4)
@@ -101,18 +105,20 @@ def tile_moe_rec_mlp_relu2_kernel(
         def gather(dst, window, lo, hi):
             nc.vector.tensor_copy(dst[:, lo:hi], window.indirect(offs_t[:, lo // 16 : hi // 16]))
 
-        cuts = [(0, 384), (384, 768), (768, 1024)]
+        cuts = [(768, 1024), (0, 384), (384, 768)]
         for lo, hi in cuts:
             gather(xw, xw_win[:].bitcast(U32), lo, hi)
         for lo, hi in cuts:
             gather(ds[0], ds_win[:], lo, hi)
         for r in range(4):
             nc.sync.dma_start(ds[1][r:P:32, :].bitcast(I32), ds[0][4 + r : P : 32, :].bitcast(I32))
-        for h in range(4):
+        for h in (3, 0, 1):
             load_words(w2[h][:], w2t_words[2 * h : 2 * h + 2])
+        for m in range(2):
+            load_words(w2[2][:, 2 * m : 2 * m + 2, :], w2t_words[4 + m : 5 + m])
 
-        nc.tensor.transpose(banks[7][:, 0:P], gate_rows[:], ident[:])
-        nc.scalar.copy(gate_col[:], banks[7][:, 0:E])
+        nc.tensor.transpose(banks[5][:, 0:P], gate_rows[:], ident[:])
+        nc.scalar.copy(gate_col[:], banks[5][:, 0:E])
 
         def slots(e):
             return slice(e * C, (e + 1) * C)
@@ -132,11 +138,10 @@ def tile_moe_rec_mlp_relu2_kernel(
 
         w1ts = w1s
         load_scales(w1ts, w1t_scales)
-        for g, members in enumerate(groups):
-            load_words(w1t[g][:], w1t_words[members[0] : members[-1] + 1])
-            if g == 0:
-                nc.sync.dma_start(pos1_t[:], pos1)
-                nc.sync.dma_start(pos2_t[:], pos2)
+        load_words(w1t[0][:], w1t_words[0:4])
+        nc.sync.dma_start(pos1_t[:], pos1)
+        nc.sync.dma_start(pos2_t[:], pos2)
+        load_words(w1t[1][:], w1t_words[4:8])
 
         def make_dh(e):
             for s in range(2):
@@ -157,20 +162,29 @@ def tile_moe_rec_mlp_relu2_kernel(
                     MULT, MULT,
                 )
 
-        lot_of = {e: (g, m) for g, members in enumerate(lots) for m, e in enumerate(members)}
-        group_of = {e: (g, m) for g, members in enumerate(groups) for m, e in enumerate(members)}
+        def make_da_aside(e):
+            nc.scalar.activation(
+                dh_gated[e][:].rearrange("c (u p d) -> c u p d", u=2, d=2),
+                banks[e][:].rearrange("c (p u d) -> c u p d", u=2, d=2),
+                ACT.Copy, scale=gate_col[:, e : e + 1],
+            )
+            nc.gpsimd.tensor_tensor(da[e][:], dh_gated[e][:], slope[e][:], MULT)
 
-        def turn(experts):
-            bank = banks[experts[0]]
+        lot_of = {e: (g, m) for g, members in enumerate(lots) for m, e in enumerate(members)}
+
+        def turn(experts, bank, at=0):
             for j, e in enumerate(experts):
                 words = da[e][:].bitcast(F32)
                 for u in range(2):
-                    nc.tensor.transpose(bank[:, (2 * j + u) * C : (2 * j + u + 1) * C], words[:, u * P : (u + 1) * P], ident[:])
+                    lo = at + (2 * j + u) * C
+                    nc.tensor.transpose(bank[:, lo : lo + C], words[:, u * P : (u + 1) * P], ident[:])
+
+        def weave(experts, bank, copy, at=0):
             g, m = lot_of[experts[0]]
             width = len(experts) * 2 * C
-            nc.scalar.copy(
+            copy(
                 da_t[g][:].bitcast(F32)[:, m * 2 * C : m * 2 * C + width].rearrange("p (m c u) -> p m c u", c=C, u=2),
-                bank[:, 0:width].rearrange("p (m u c) -> p m c u", c=C, u=2),
+                bank[:, at : at + width].rearrange("p (m u c) -> p m c u", c=C, u=2),
             )
 
         def quantize(g):
@@ -178,52 +192,53 @@ def tile_moe_rec_mlp_relu2_kernel(
 
         def dx_product(e, kt, dst):
             g, m = lot_of[e]
-            wg, wm = group_of[e]
             nc.tensor.matmul_mx(
                 dst,
-                lhsT=w1t[wg][:, wm, 2 * P * kt : 2 * P * (kt + 1)].bitcast(FP4X4),
+                lhsT=w1t[e // 4][:, e % 4, 2 * P * kt : 2 * P * (kt + 1)].bitcast(FP4X4),
                 lhsT_scale=w1ts[:, e, kt * P : (kt + 1) * P],
                 rhs=da_codes[g][:, slots(m)].bitcast(FP8X4),
                 rhs_scale=da_scales[g][:, slots(m)], start=True, stop=True,
             )
 
-        def make_dx(experts, row_tiles, bank, copies):
-            width = len(experts) * C
-            for e in experts:
-                for j, kt in enumerate(row_tiles):
-                    at = j * width + (e - experts[0]) * C
-                    dx_product(e, kt, bank[:, at : at + C])
-            for j, kt in enumerate(row_tiles):
-                copies[j](dx[kt][:, experts[0] * C : experts[0] * C + width], bank[:, j * width : (j + 1) * width])
+        def dx_products(experts, kt, bank):
+            for j, e in enumerate(experts):
+                dx_product(e, kt, bank[:, slots(j)])
+
+        def dx_out(experts, kt, bank, copy):
+            copy(dx[kt][:, experts[0] * C : (experts[-1] + 1) * C], bank[:, 0 : len(experts) * C])
+
+        def make_dx(experts, kt, bank, copy):
+            dx_products(experts, kt, bank)
+            dx_out(experts, kt, bank, copy)
 
         on_scalar, on_vector = nc.scalar.copy, nc.vector.tensor_copy
+
+        def turn_pair(first, bank):
+            turn((first, first + 1), bank)
+            weave((first, first + 1), bank, on_scalar)
 
         for lo, hi in cuts:
             for s in range(2):
                 gather(dw[s], dw_win[:, s, :].bitcast(U32), lo, hi)
-        for e in range(E):
-            make_dh(e)
-        for first in (0, 2, 4):
-            make_da(first)
-            make_da(first + 1)
-            turn((first, first + 1))
+            for e in range(lo // C, hi // C):
+                make_dh(e)
+        make_da_aside(6)
+        make_da_aside(7)
+        for e in range(6):
+            make_da(e)
+        for first, b in ((0, 0), (2, 2), (6, 3), (4, 4)):
+            turn_pair(first, banks[b])
         quantize(0)
-        make_da(6)
-        turn((6,))
-        make_da(7)
-        turn((7,))
-        for kt, b in enumerate((1, 3, 0, 2)):
-            make_dx(groups[0], (kt,), banks[b], (on_scalar,))
-        for g in range(1, 4):
-            quantize(g)
-        make_dx(groups[1], (0, 1), banks[5], (on_vector, on_vector))
-        make_dx(groups[1], (2, 3), banks[4], (on_vector, on_vector))
-        make_dx(groups[2], (0, 1), banks[6], (on_scalar, on_vector))
-        make_dx(groups[2], (2, 3), banks[7], (on_vector, on_vector))
+        quantize(1)
+        for kt, b in enumerate((1, 6, 7, 0)):
+            make_dx((0, 1, 2, 3), kt, banks[b], on_scalar if kt < 3 else on_vector)
+        for kt, b in enumerate((5, 2, 3, 4)):
+            make_dx((4, 5, 6, 7), kt, banks[b], on_vector if kt < 3 else on_scalar)
 
         halves = [(0, T // 2), (T // 2, T)]
+        last_cuts = [(0, T // 2), (T // 2, 3 * T // 4), (3 * T // 4, T)]
         for kt in range(ROW_TILES):
-            for lo, hi in halves:
+            for lo, hi in halves if kt < ROW_TILES - 1 else last_cuts:
                 nc.scalar.activation(first_pick[kt][:, lo:hi], dx[kt][:].indirect(pos1_t[:, lo // 16 : hi // 16]), ACT.Copy)
                 nc.vector.tensor_tensor(
                     total[kt][:, lo:hi], dx[kt][:].indirect(pos2_t[:, lo // 16 : hi // 16]), first_pick[kt][:, lo:hi], ADD

@@ -52,7 +52,8 @@ def tile_moe_rec_mlp_relu2_kernel(
         ident = held([P, P], F32, "ident")
         w1 = [held([P, 4, 2 * H], U8, "w1_%d" % h) for h in range(2)]
         w2 = [held([P, 4, 2 * H], U8, "w2_%d" % h) for h in range(4)]
-        w1t = [held([P, 4, 2 * K], U8, "w1t_%d" % h) for h in range(2)]
+        w1t_early = held([P, 4, 2 * K], U8, "w1t_early")
+        w1t_late = [held([P, 4, K], U8, "w1t_late%d" % h) for h in range(2)]
         w1s = held([P, E, H], U8, "w1s")
         w2s = held([P, 2 * E, H], U8, "w2s")
         slope = [held([P, H], F32, "slope%d" % e) for e in range(E)]
@@ -138,10 +139,16 @@ def tile_moe_rec_mlp_relu2_kernel(
 
         w1ts = w1s
         load_scales(w1ts, w1t_scales)
-        load_words(w1t[0][:], w1t_words[0:4])
         nc.sync.dma_start(pos1_t[:], pos1)
         nc.sync.dma_start(pos2_t[:], pos2)
-        load_words(w1t[1][:], w1t_words[4:8])
+        load_words(w1t_early[:], w1t_words[0:4])
+        for h in range(2):
+            load_words(w1t_late[h][:], w1t_words[4:8, :, :, h * K : (h + 1) * K])
+
+        def w1t_columns(e, kt):
+            if e < 4:
+                return w1t_early[:, e, 2 * P * kt : 2 * P * (kt + 1)]
+            return w1t_late[kt // 2][:, e - 4, 2 * P * (kt % 2) : 2 * P * (kt % 2 + 1)]
 
         def make_dh(e):
             for s in range(2):
@@ -194,7 +201,7 @@ def tile_moe_rec_mlp_relu2_kernel(
             g, m = lot_of[e]
             nc.tensor.matmul_mx(
                 dst,
-                lhsT=w1t[e // 4][:, e % 4, 2 * P * kt : 2 * P * (kt + 1)].bitcast(FP4X4),
+                lhsT=w1t_columns(e, kt).bitcast(FP4X4),
                 lhsT_scale=w1ts[:, e, kt * P : (kt + 1) * P],
                 rhs=da_codes[g][:, slots(m)].bitcast(FP8X4),
                 rhs_scale=da_scales[g][:, slots(m)], start=True, stop=True,
@@ -230,10 +237,11 @@ def tile_moe_rec_mlp_relu2_kernel(
             turn_pair(first, banks[b])
         quantize(0)
         quantize(1)
-        for kt, b in enumerate((1, 6, 7, 0)):
-            make_dx((0, 1, 2, 3), kt, banks[b], on_scalar if kt < 3 else on_vector)
-        for kt, b in enumerate((5, 2, 3, 4)):
-            make_dx((4, 5, 6, 7), kt, banks[b], on_vector if kt < 3 else on_scalar)
+        for first, late_banks in ((0, (5, 2)), (2, (3, 4))):
+            for j, b in enumerate((1, 6)):
+                make_dx((0, 1, 2, 3), first + j, banks[b], on_scalar)
+            for j, b in enumerate(late_banks):
+                make_dx((4, 5, 6, 7), first + j, banks[b], on_vector)
 
         halves = [(0, T // 2), (T // 2, T)]
         last_cuts = [(0, T // 2), (T // 2, 3 * T // 4), (3 * T // 4, T)]

@@ -58,7 +58,6 @@ def tile_moe_rec_mlp_relu2_kernel(
         w2s = held([P, 2 * E, H], U8, "w2s")
         slope = [held([P, H], F32, "slope%d" % e) for e in range(E)]
         da = [held([P, H], BF16, "da%d" % e) for e in range(E)]
-        dh_gated = {e: held([P, H], F32, "dh_gated%d" % e) for e in (6, 7)}
         lots = [(0, 1, 2, 3), (4, 5, 6, 7)]
         da_t = [held([P, len(g) * C * 4], BF16, "da_t%d" % g[0]) for g in lots]
         da_codes = [held([P, len(g) * C], U32, "da_codes%d" % g[0]) for g in lots]
@@ -138,10 +137,11 @@ def tile_moe_rec_mlp_relu2_kernel(
                 )
 
         w1ts = w1s
-        load_scales(w1ts, w1t_scales)
+        load_scales(w1ts[:, 0:4, :], w1t_scales[0:4])
         nc.sync.dma_start(pos1_t[:], pos1)
         nc.sync.dma_start(pos2_t[:], pos2)
         load_words(w1t_early[:], w1t_words[0:4])
+        load_scales(w1ts[:, 4:8, :], w1t_scales[4:8])
         for h in range(2):
             load_words(w1t_late[h][:], w1t_words[4:8, :, :, h * K : (h + 1) * K])
 
@@ -150,10 +150,12 @@ def tile_moe_rec_mlp_relu2_kernel(
                 return w1t_early[:, e, 2 * P * kt : 2 * P * (kt + 1)]
             return w1t_late[kt // 2][:, e - 4, 2 * P * (kt % 2) : 2 * P * (kt % 2 + 1)]
 
+        dh_banks = {e: banks[{3: 6, 4: 0, 5: 2}.get(e, e)] for e in range(E)}
+
         def make_dh(e):
             for s in range(2):
                 nc.tensor.matmul_mx(
-                    banks[e][:], lhsT=dw[s][:, slots(e)].bitcast(FP8X4), lhsT_scale=ds[s][:, slots(e)],
+                    dh_banks[e][:], lhsT=dw[s][:, slots(e)].bitcast(FP8X4), lhsT_scale=ds[s][:, slots(e)],
                     rhs=w2[e // 2][:, 2 * (e % 2) + s, :].bitcast(FP4X4), rhs_scale=w2s[:, 2 * e + s, :],
                     start=(s == 0), stop=(s == 1),
                 )
@@ -163,19 +165,11 @@ def tile_moe_rec_mlp_relu2_kernel(
                 half = slice(u * 2 * P, (u + 1) * 2 * P)
                 nc.vector.scalar_tensor_tensor(
                     da[e][:, half].rearrange("c (p d) -> c p d", d=2),
-                    banks[e][:].rearrange("c (p u d) -> c u p d", u=2, d=2)[:, u],
+                    dh_banks[e][:].rearrange("c (p u d) -> c u p d", u=2, d=2)[:, u],
                     gate_col[:, e : e + 1],
                     slope[e][:, half].rearrange("c (p d) -> c p d", d=2),
                     MULT, MULT,
                 )
-
-        def make_da_aside(e):
-            nc.scalar.activation(
-                dh_gated[e][:].rearrange("c (u p d) -> c u p d", u=2, d=2),
-                banks[e][:].rearrange("c (p u d) -> c u p d", u=2, d=2),
-                ACT.Copy, scale=gate_col[:, e : e + 1],
-            )
-            nc.gpsimd.tensor_tensor(da[e][:], dh_gated[e][:], slope[e][:], MULT)
 
         lot_of = {e: (g, m) for g, members in enumerate(lots) for m, e in enumerate(members)}
 
@@ -227,21 +221,29 @@ def tile_moe_rec_mlp_relu2_kernel(
         for lo, hi in cuts:
             for s in range(2):
                 gather(dw[s], dw_win[:, s, :].bitcast(U32), lo, hi)
-            for e in range(lo // C, hi // C):
-                make_dh(e)
-        make_da_aside(6)
-        make_da_aside(7)
-        for e in range(6):
-            make_da(e)
-        for first, b in ((0, 0), (2, 2), (6, 3), (4, 4)):
-            turn_pair(first, banks[b])
+        for e in (6, 7, 0, 1, 2):
+            make_dh(e)
+        make_da(6)
+        make_dh(3)
+        make_da(7)
+        make_da(0)
+        make_dh(4)
+        make_da(1)
+        turn_pair(0, banks[3])
+        make_da(2)
+        make_dh(5)
+        make_da(3)
+        turn_pair(2, banks[4])
+        turn_pair(6, banks[6])
+        make_da(4)
+        make_da(5)
+        turn_pair(4, banks[5])
         quantize(0)
         quantize(1)
-        for first, late_banks in ((0, (5, 2)), (2, (3, 4))):
-            for j, b in enumerate((1, 6)):
-                make_dx((0, 1, 2, 3), first + j, banks[b], on_scalar)
-            for j, b in enumerate(late_banks):
-                make_dx((4, 5, 6, 7), first + j, banks[b], on_vector)
+        for kt, b in enumerate((7, 3, 1, 4)):
+            make_dx((0, 1, 2, 3), kt, banks[b], on_scalar if kt < 3 else on_vector)
+        for kt, b in enumerate((0, 2, 6, 5)):
+            make_dx((4, 5, 6, 7), kt, banks[b], on_vector if kt < 3 else on_scalar)
 
         halves = [(0, T // 2), (T // 2, T)]
         last_cuts = [(0, T // 2), (T // 2, 3 * T // 4), (3 * T // 4, T)]

@@ -58,7 +58,7 @@ def tile_moe_rec_mlp_relu2_kernel(
         w2s = held([P, 2 * E, H], U8, "w2s")
         slope = [held([P, H], F32, "slope%d" % e) for e in range(E)]
         da = [held([P, H], BF16, "da%d" % e) for e in range(E)]
-        lots = [(0, 1, 2, 3), (4, 5, 6, 7)]
+        lots = [(0, 1, 2, 3), (4, 5), (6,), (7,)]
         da_t = [held([P, len(g) * C * 4], BF16, "da_t%d" % g[0]) for g in lots]
         da_codes = [held([P, len(g) * C], U32, "da_codes%d" % g[0]) for g in lots]
         da_scales = [held([P, len(g) * C], U8, "da_scales%d" % g[0]) for g in lots]
@@ -105,20 +105,20 @@ def tile_moe_rec_mlp_relu2_kernel(
         def gather(dst, window, lo, hi):
             nc.vector.tensor_copy(dst[:, lo:hi], window.indirect(offs_t[:, lo // 16 : hi // 16]))
 
-        cuts = [(768, 1024), (0, 384), (384, 768)]
+        cuts = [(0, 256), (256, 640), (640, 1024)]
         for lo, hi in cuts:
             gather(xw, xw_win[:].bitcast(U32), lo, hi)
         for lo, hi in cuts:
             gather(ds[0], ds_win[:], lo, hi)
         for r in range(4):
             nc.sync.dma_start(ds[1][r:P:32, :].bitcast(I32), ds[0][4 + r : P : 32, :].bitcast(I32))
-        for h in (3, 0, 1):
+        for h in range(3):
             load_words(w2[h][:], w2t_words[2 * h : 2 * h + 2])
         for m in range(2):
-            load_words(w2[2][:, 2 * m : 2 * m + 2, :], w2t_words[4 + m : 5 + m])
+            load_words(w2[3][:, 2 * m : 2 * m + 2, :], w2t_words[6 + m : 7 + m])
 
-        nc.tensor.transpose(banks[5][:, 0:P], gate_rows[:], ident[:])
-        nc.scalar.copy(gate_col[:], banks[5][:, 0:E])
+        nc.tensor.transpose(banks[7][:, 0:P], gate_rows[:], ident[:])
+        nc.scalar.copy(gate_col[:], banks[7][:, 0:E])
 
         def slots(e):
             return slice(e * C, (e + 1) * C)
@@ -150,7 +150,7 @@ def tile_moe_rec_mlp_relu2_kernel(
                 return w1t_early[:, e, 2 * P * kt : 2 * P * (kt + 1)]
             return w1t_late[kt // 2][:, e - 4, 2 * P * (kt % 2) : 2 * P * (kt % 2 + 1)]
 
-        dh_banks = {e: banks[{3: 6, 4: 0, 5: 2}.get(e, e)] for e in range(E)}
+        dh_banks = {e: banks[{6: 3, 7: 5}.get(e, e)] for e in range(E)}
 
         def make_dh(e):
             for s in range(2):
@@ -214,43 +214,50 @@ def tile_moe_rec_mlp_relu2_kernel(
 
         on_scalar, on_vector = nc.scalar.copy, nc.vector.tensor_copy
 
-        def turn_pair(first, bank):
-            turn((first, first + 1), bank)
-            weave((first, first + 1), bank, on_scalar)
+        def turn_out(experts, bank):
+            turn(experts, bank)
+            weave(experts, bank, on_scalar)
 
         for lo, hi in cuts:
             for s in range(2):
                 gather(dw[s], dw_win[:, s, :].bitcast(U32), lo, hi)
-        for e in (6, 7, 0, 1, 2):
+        for e in range(6):
             make_dh(e)
-        make_da(6)
-        make_dh(3)
-        make_da(7)
-        make_da(0)
-        make_dh(4)
-        make_da(1)
-        turn_pair(0, banks[3])
-        make_da(2)
-        make_dh(5)
+        for e in range(3):
+            make_da(e)
+        turn_out((0, 1), banks[2])
         make_da(3)
-        turn_pair(2, banks[4])
-        turn_pair(6, banks[6])
+        turn_out((2, 3), banks[6])
+        make_dh(6)
         make_da(4)
         make_da(5)
-        turn_pair(4, banks[5])
-        quantize(0)
-        quantize(1)
-        for kt, b in enumerate((7, 3, 1, 4)):
-            make_dx((0, 1, 2, 3), kt, banks[b], on_scalar if kt < 3 else on_vector)
-        for kt, b in enumerate((0, 2, 6, 5)):
-            make_dx((4, 5, 6, 7), kt, banks[b], on_vector if kt < 3 else on_scalar)
+        make_dh(7)
+        turn_out((4, 5), banks[7])
+        make_da(6)
+        turn_out((6,), banks[0])
+        make_da(7)
+        turn_out((7,), banks[1])
+        for g in range(len(lots)):
+            quantize(g)
+        make_dx((0, 1, 2, 3), 0, banks[4], on_scalar)
+        make_dx((0, 1, 2, 3), 1, banks[2], on_scalar)
+        make_dx((4, 5), 0, banks[6], on_vector)
+        make_dx((6, 7), 0, banks[3], on_vector)
+        make_dx((4, 5, 6, 7), 1, banks[5], on_vector)
 
-        halves = [(0, T // 2), (T // 2, T)]
-        last_cuts = [(0, T // 2), (T // 2, 3 * T // 4), (3 * T // 4, T)]
-        for kt in range(ROW_TILES):
-            for lo, hi in halves if kt < ROW_TILES - 1 else last_cuts:
+        def combine(kt, pieces):
+            for lo, hi in pieces:
                 nc.scalar.activation(first_pick[kt][:, lo:hi], dx[kt][:].indirect(pos1_t[:, lo // 16 : hi // 16]), ACT.Copy)
                 nc.vector.tensor_tensor(
                     total[kt][:, lo:hi], dx[kt][:].indirect(pos2_t[:, lo // 16 : hi // 16]), first_pick[kt][:, lo:hi], ADD
                 )
                 nc.sync.dma_start(out[kt * P : (kt + 1) * P, lo:hi], total[kt][:, lo:hi])
+
+        halves = [(0, T // 2), (T // 2, T)]
+        combine(0, halves)
+        for kt, early, late in ((2, 6, 7), (3, 3, 0)):
+            make_dx((0, 1, 2, 3), kt, banks[early], on_scalar)
+            make_dx((4, 5, 6, 7), kt, banks[late], on_vector)
+        combine(1, halves)
+        combine(2, halves)
+        combine(3, [(0, T // 2), (T // 2, 3 * T // 4), (3 * T // 4, T)])

@@ -239,11 +239,14 @@ def tile_moe_rec_mlp_relu2_kernel(
         turn_out((7,), banks[1])
         for g in range(len(lots)):
             quantize(g)
-        make_dx((0, 1, 2, 3), 0, banks[4], on_scalar)
-        make_dx((0, 1, 2, 3), 1, banks[2], on_scalar)
-        make_dx((4, 5), 0, banks[6], on_vector)
-        make_dx((6, 7), 0, banks[3], on_vector)
-        make_dx((4, 5, 6, 7), 1, banks[5], on_vector)
+        early, late = (0, 1, 2, 3), (4, 5, 6, 7)
+        make_dx(early, 0, banks[2], on_scalar)
+        make_dx(early, 1, banks[4], on_vector)
+        make_dx(early, 2, banks[6], on_scalar)
+        make_dx(early, 3, banks[3], on_vector)
+        make_dx(late, 0, banks[7], on_scalar)
+        make_dx(late, 1, banks[5], on_vector)
+        make_dx(late, 2, banks[0], on_vector)
 
         def combine(kt, pieces):
             for lo, hi in pieces:
@@ -255,9 +258,7 @@ def tile_moe_rec_mlp_relu2_kernel(
 
         halves = [(0, T // 2), (T // 2, T)]
         combine(0, halves)
-        for kt, early, late in ((2, 6, 7), (3, 3, 0)):
-            make_dx((0, 1, 2, 3), kt, banks[early], on_scalar)
-            make_dx((4, 5, 6, 7), kt, banks[late], on_vector)
         combine(1, halves)
+        make_dx(late, 3, banks[1], on_scalar)
         combine(2, halves)
         combine(3, [(0, T // 2), (T // 2, 3 * T // 4), (3 * T // 4, T)])

from contextlib import ExitStack

import concourse.mybir as mybir
from concourse.masks import make_identity

K, T, E, C, H, N = 512, 512, 8, 128, 512, 1024
S = E * C
P = 128
ROW_TILES = K // P
FLOPS = 2 * S * (K * H + N * H + H * K)

F32 = mybir.dt.float32
BF16 = mybir.dt.bfloat16
I32 = mybir.dt.int32
U32 = mybir.dt.uint32
U16 = mybir.dt.uint16
U8 = mybir.dt.uint8
FP8X4 = mybir.dt.float8_e4m3fn_x4
FP4X4 = mybir.dt.float4_e2m1fn_x4
MULT = mybir.AluOpType.mult
ADD = mybir.AluOpType.add
ACT = mybir.ActivationFunctionType


def tile_moe_rec_mlp_relu2_kernel(
    tc, x_words, x_scales, dy_words, dy_scales, w1_words, w1_scales, w2t_words, w2t_scales,
    w1t_words, w1t_scales, gate, offs, pos1, pos2, out,
):
    nc = tc.nc
    with ExitStack() as ctx:
        keep = ctx.enter_context(tc.tile_pool(name="keep", bufs=1))
        psum = ctx.enter_context(tc.psum_pool(name="psum", bufs=1))

        def held(shape, dtype, name):
            return keep.tile(shape, dtype, name=name, align_bytes=64)

        banks = [psum.tile([P, 512], F32, name="bank%d" % b) for b in range(8)]

        offs_t = held([P, S // 16], U16, "offs_t")
        pos1_t = held([P, T // 16], U16, "pos1_t")
        pos2_t = held([P, T // 16], U16, "pos2_t")
        xw_win = held([P, T], I32, "xw_win")
        xs_win = held([P, T], U8, "xs_win")
        dw_win = held([P, 2, T], I32, "dw_win")
        ds_win = held([P, T], U8, "ds_win")
        xw = held([P, S], U32, "xw")
        xs = held([P, S], U8, "xs")
        dw = [held([P, S], U32, "dw%d" % s) for s in range(2)]
        ds = [held([P, S], U8, "ds%d" % s) for s in range(2)]
        gate_rows = held([P, C], F32, "gate_rows")
        gate_col = held([P, E], F32, "gate_col")
        ident = held([P, P], F32, "ident")
        w1 = [held([P, 4, 2 * H], U8, "w1_%d" % h) for h in range(2)]
        w2 = [held([P, 4, 2 * H], U8, "w2_%d" % h) for h in range(4)]
        w1t_early = held([P, 4, 2 * K], U8, "w1t_early")
        w1t_late = [held([P, 4, K], U8, "w1t_late%d" % h) for h in range(2)]
        w1s = held([P, E, H], U8, "w1s")
        w2s = held([P, 2 * E, H], U8, "w2s")
        slope = [held([P, H], F32, "slope%d" % e) for e in range(E)]
        da = [held([P, H], BF16, "da%d" % e) for e in range(E)]
        lots = [(0, 1, 2, 3), (4, 5), (6,), (7,)]
        da_t = [held([P, len(g) * C * 4], BF16, "da_t%d" % g[0]) for g in lots]
        da_codes = [held([P, len(g) * C], U32, "da_codes%d" % g[0]) for g in lots]
        da_scales = [held([P, len(g) * C], U8, "da_scales%d" % g[0]) for g in lots]
        dx = [held([P, S], F32, "dx%d" % kt) for kt in range(ROW_TILES)]
        first_pick = [held([P, T], F32, "first_pick%d" % kt) for kt in range(ROW_TILES)]
        total = [held([P, T], F32, "total%d" % kt) for kt in range(ROW_TILES)]

        def zero(engine, plane):
            engine.memset(plane.bitcast(I32), 0)

        zero(nc.gpsimd, ds_win[:])
        zero(nc.gpsimd, xs_win[:])
        make_identity(nc, ident[:])
        zero(nc.gpsimd, ds[1][:])
        nc.vector.memset(gate_rows[:], 0.0)
        zero(nc.vector, w1s[:].rearrange("p e n -> p (e n)"))
        for h in range(2):
            nc.scalar.copy(
                w2s[:, h * E : (h + 1) * E, :].rearrange("p e n -> p (e n)").bitcast(U32),
                w1s[:].rearrange("p e n -> p (e n)").bitcast(U32),
            )

        def load_scales(plane, rows):
            by_row = rows.rearrange("e s (q r) n -> r q (e s) n", r=4)
            for r in range(4):
                nc.sync.dma_start(plane[r:P:32, :, :].bitcast(I32), by_row[r].bitcast(I32))

        def load_words(tile, words):
            nc.sync.dma_start(tile.bitcast(I32), words.rearrange("e s p b -> p (e s) b").bitcast(I32))

        nc.sync.dma_start(offs_t[:], offs)
        nc.sync.dma_start(xw_win[:], x_words[0].rearrange("p t d -> p (t d)").bitcast(I32))
        for q in range(4):
            nc.sync.dma_start(ds_win[32 * q : 32 * q + 8, :].bitcast(I32), dy_scales[:, 4 * q : 4 * q + 4, :].bitcast(I32))
        load_words(w1[0][:], w1_words[0:4])
        load_words(w1[1][:], w1_words[4:8])
        for q in range(4):
            nc.sync.dma_start(xs_win[32 * q : 32 * q + 4, :].bitcast(I32), x_scales[0, 4 * q : 4 * q + 4, :].bitcast(I32))
        nc.sync.dma_start(dw_win[:], dy_words.rearrange("s p t d -> p s (t d)").bitcast(I32))
        nc.sync.dma_start(gate_rows[0:E, :], gate[0, :].rearrange("(e c) -> e c", c=C))
        load_scales(w1s, w1_scales)
        load_scales(w2s, w2t_scales)

        def gather(dst, window, lo, hi):
            nc.vector.tensor_copy(dst[:, lo:hi], window.indirect(offs_t[:, lo // 16 : hi // 16]))

        cuts = [(0, 256), (256, 640), (640, 1024)]
        for lo, hi in cuts:
            gather(xw, xw_win[:].bitcast(U32), lo, hi)
        for lo, hi in cuts:
            gather(ds[0], ds_win[:], lo, hi)
        for r in range(4):
            nc.sync.dma_start(ds[1][r:P:32, :].bitcast(I32), ds[0][4 + r : P : 32, :].bitcast(I32))
        for h in range(3):
            load_words(w2[h][:], w2t_words[2 * h : 2 * h + 2])
        for m in range(2):
            load_words(w2[3][:, 2 * m : 2 * m + 2, :], w2t_words[6 + m : 7 + m])

        nc.tensor.transpose(banks[7][:, 0:P], gate_rows[:], ident[:])
        nc.scalar.copy(gate_col[:], banks[7][:, 0:E])

        def slots(e):
            return slice(e * C, (e + 1) * C)

        for lo, hi in cuts:
            gather(xs, xs_win[:], lo, hi)
            for e in range(lo // C, hi // C):
                nc.tensor.matmul_mx(
                    banks[e][:], lhsT=xw[:, slots(e)].bitcast(FP8X4), lhsT_scale=xs[:, slots(e)],
                    rhs=w1[e // 4][:, e % 4, :].bitcast(FP4X4), rhs_scale=w1s[:, e, :], start=True, stop=True,
                )
                nc.scalar.activation(
                    slope[e][:].rearrange("c (u p d) -> c u p d", u=2, d=2),
                    banks[e][:].rearrange("c (p u d) -> c u p d", u=2, d=2),
                    ACT.Relu, scale=2.0,
                )

        w1ts = w1s
        load_scales(w1ts[:, 0:4, :], w1t_scales[0:4])
        nc.sync.dma_start(pos1_t[:], pos1)
        nc.sync.dma_start(pos2_t[:], pos2)
        load_words(w1t_early[:], w1t_words[0:4])
        load_scales(w1ts[:, 4:8, :], w1t_scales[4:8])
        for h in range(2):
            load_words(w1t_late[h][:], w1t_words[4:8, :, :, h * K : (h + 1) * K])

        def w1t_columns(e, kt):
            if e < 4:
                return w1t_early[:, e, 2 * P * kt : 2 * P * (kt + 1)]
            return w1t_late[kt // 2][:, e - 4, 2 * P * (kt % 2) : 2 * P * (kt % 2 + 1)]

        dh_banks = {e: banks[{6: 3, 7: 5}.get(e, e)] for e in range(E)}

        def make_dh(e):
            for s in range(2):
                nc.tensor.matmul_mx(
                    dh_banks[e][:], lhsT=dw[s][:, slots(e)].bitcast(FP8X4), lhsT_scale=ds[s][:, slots(e)],
                    rhs=w2[e // 2][:, 2 * (e % 2) + s, :].bitcast(FP4X4), rhs_scale=w2s[:, 2 * e + s, :],
                    start=(s == 0), stop=(s == 1),
                )

        def make_da(e):
            for u in range(2):
                half = slice(u * 2 * P, (u + 1) * 2 * P)
                nc.vector.scalar_tensor_tensor(
                    da[e][:, half].rearrange("c (p d) -> c p d", d=2),
                    dh_banks[e][:].rearrange("c (p u d) -> c u p d", u=2, d=2)[:, u],
                    gate_col[:, e : e + 1],
                    slope[e][:, half].rearrange("c (p d) -> c p d", d=2),
                    MULT, MULT,
                )

        lot_of = {e: (g, m) for g, members in enumerate(lots) for m, e in enumerate(members)}

        def turn(experts, bank, at=0):
            for j, e in enumerate(experts):
                words = da[e][:].bitcast(F32)
                for u in range(2):
                    lo = at + (2 * j + u) * C
                    nc.tensor.transpose(bank[:, lo : lo + C], words[:, u * P : (u + 1) * P], ident[:])

        def weave(experts, bank, copy, at=0):
            g, m = lot_of[experts[0]]
            width = len(experts) * 2 * C
            copy(
                da_t[g][:].bitcast(F32)[:, m * 2 * C : m * 2 * C + width].rearrange("p (m c u) -> p m c u", c=C, u=2),
                bank[:, at : at + width].rearrange("p (m u c) -> p m c u", c=C, u=2),
            )

        def quantize(g):
            nc.vector.quantize_mx(da_codes[g][:].bitcast(FP8X4), da_scales[g][:], da_t[g][:])

        def dx_product(e, kt, dst):
            g, m = lot_of[e]
            nc.tensor.matmul_mx(
                dst,
                lhsT=w1t_columns(e, kt).bitcast(FP4X4),
                lhsT_scale=w1ts[:, e, kt * P : (kt + 1) * P],
                rhs=da_codes[g][:, slots(m)].bitcast(FP8X4),
                rhs_scale=da_scales[g][:, slots(m)], start=True, stop=True,
            )

        def dx_products(experts, kt, bank):
            for j, e in enumerate(experts):
                dx_product(e, kt, bank[:, slots(j)])

        def dx_out(experts, kt, bank, copy):
            copy(dx[kt][:, experts[0] * C : (experts[-1] + 1) * C], bank[:, 0 : len(experts) * C])

        def make_dx(experts, kt, bank, copy):
            dx_products(experts, kt, bank)
            dx_out(experts, kt, bank, copy)

        on_scalar, on_vector = nc.scalar.copy, nc.vector.tensor_copy

        def turn_out(experts, bank):
            turn(experts, bank)
            weave(experts, bank, on_scalar)

        for lo, hi in cuts:
            for s in range(2):
                gather(dw[s], dw_win[:, s, :].bitcast(U32), lo, hi)
        for e in range(6):
            make_dh(e)
        for e in range(3):
            make_da(e)
        turn_out((0, 1), banks[2])
        make_da(3)
        turn_out((2, 3), banks[6])
        make_dh(6)
        make_da(4)
        make_da(5)
        make_dh(7)
        turn_out((4, 5), banks[7])
        make_da(6)
        turn_out((6,), banks[0])
        make_da(7)
        turn_out((7,), banks[1])
        for g in range(len(lots)):
            quantize(g)
        early, late = (0, 1, 2, 3), (4, 5, 6, 7)
        make_dx(early, 0, banks[2], on_scalar)
        make_dx(early, 1, banks[4], on_vector)
        make_dx(early, 2, banks[6], on_scalar)
        make_dx(early, 3, banks[3], on_vector)
        make_dx(late, 0, banks[7], on_scalar)
        make_dx(late, 1, banks[5], on_vector)
        make_dx(late, 2, banks[0], on_vector)

        def combine(kt, pieces):
            for lo, hi in pieces:
                nc.scalar.activation(first_pick[kt][:, lo:hi], dx[kt][:].indirect(pos1_t[:, lo // 16 : hi // 16]), ACT.Copy)
                nc.vector.tensor_tensor(
                    total[kt][:, lo:hi], dx[kt][:].indirect(pos2_t[:, lo // 16 : hi // 16]), first_pick[kt][:, lo:hi], ADD
                )
                nc.sync.dma_start(out[kt * P : (kt + 1) * P, lo:hi], total[kt][:, lo:hi])

        halves = [(0, T // 2), (T // 2, T)]
        combine(0, halves)
        combine(1, halves)
        make_dx(late, 3, banks[1], on_scalar)
        combine(2, halves)
        combine(3, [(0, T // 2), (T // 2, 3 * T // 4), (3 * T // 4, T)])
